import numpy as np, ml_dtypes
CORES = [16,17,18,19,32,33,34,35]
N = 8
import mx_ref
BF = ml_dtypes.bfloat16
def pick(q, e):
    c = np.concatenate([q[0].reshape(128, -1, 4), np.zeros((128, 1, 4), np.uint8)], axis=1); s = np.concatenate([q[1], np.ones((16, 1), np.uint8)], axis=1)
    return (np.ascontiguousarray(c[:, e].reshape(128, -1)), np.ascontiguousarray(s[:, e]))
def join(*qs):
    return (np.concatenate([q[0] for q in qs], axis=1), np.concatenate([q[1] for q in qs], axis=1))
def put(q, e, v):
    c, s = q[0].reshape(128, -1, 4).copy(), q[1].copy(); c[:, e] = v[0].reshape(128, -1, 4); s[:, e] = v[1]
    return (c.reshape(128, -1), s)
def pk(c, s):
    return (np.ascontiguousarray(c), mx_ref.live(s))
def emit(q):
    return q[0], q[1]
def cut(t, i, w=512):
    return t[:, w * i:w * i + w]
def tile(rs):
    return np.stack(rs, axis=2).reshape(128, -1).astype(BF)
def f(rng, *shape):
    return mx_ref.flush((rng.standard_normal(shape, dtype=np.float32) * np.exp2(rng.integers(-2, 3, shape[:-1] + (1,)))).astype(BF))
def wide(rng, *shape, cols=0):
    v = rng.standard_normal(shape, dtype=np.float32) * np.exp2(rng.integers(-12, 13, shape)).astype(np.float32)
    if cols: v *= np.repeat(np.exp2(rng.integers(-cols, cols + 1, shape[:-2] + (1, shape[-1] // 4))) * (rng.random(shape[:-2] + (1, shape[-1] // 4)) > 0.0625), 4, axis=-1).astype(np.float32)
    return mx_ref.flush(v.astype(BF))
T, L, CAPP = 128, 3, 48
def game(x, u, w):
    S = [mx_ref.quantize(np.ascontiguousarray(x[r])) for r in range(N)]
    qu = [mx_ref.quantize(np.ascontiguousarray(u[r])) for r in range(N)]
    at, ks, made = np.arange(N * T).reshape(N, T), np.zeros((N, 1, L), np.float32), []
    for b in range(L):
        want = [np.flatnonzero(mx_ref.matmul(qu[r], S[r])[b] + np.float32(0) < 0) for r in range(N)]
        new, now = [], at.copy()
        for r in range(N):
            p = r ^ (1 << b)
            k = min(len(want[r]), len(want[p]), CAPP)
            to, of = want[r][:k], want[p][:k]
            c = pick(S[p], np.concatenate([of, np.full(CAPP - k, -1)]))
            t = tile([np.float32(0.0625) * mx_ref.matmul(mx_ref.quantize(np.ascontiguousarray(cut(w[r], 4 * b + i))), c) for i in range(4)])
            made.append(t)
            new.append(put(S[r], to, pick(mx_ref.quantize(t), np.arange(k))))
            now[r, to] = at[p, of]
            ks[r, 0, b] = k
        S, at = new, now
    return S, at, ks, made
def fit(t, low, high):
    a = np.abs(t.astype(np.float32))
    return bool((np.isfinite(a) & ((a == 0) | (a >= low) & (a <= high))).all())
def blocks(t):
    return np.abs(t.astype(np.float32)).reshape(16, 8, -1, 4).max(axis=(1, 3))
def plain(rng):
    u = np.array(f(rng, N, 128, 512))
    u[:, :, 4 * L:] = 0
    a = np.exp2(rng.integers(-2, 3, (N, 128, 1, 1)))
    x, lean = rng.standard_normal((N, 128, T, 4)), 2.5 * rng.random((N, L)) - 1
    for b in range(L):
        h = a * u[:, :, None, 4 * b:4 * b + 4].astype(np.float64)
        x += lean[:, b, None, None, None] * h * np.sum(h * h, axis=(1, 2, 3), keepdims=True) ** -0.5
    x = mx_ref.flush((a * x).reshape(N, 128, 4 * T).astype(np.float32).astype(BF))
    return {"x": x, "u": u, "w": f(rng, N, 128, 2048 * L), "v": f(rng, N, 128, 512)}
def aim(x, u, wish):
    x = x.reshape(N, 128, T, 4).astype(np.float32)
    for r in range(N):
        s = mx_ref.matmul(mx_ref.quantize(np.ascontiguousarray(u[r])), mx_ref.quantize(np.ascontiguousarray(x[r].reshape(128, 4 * T).astype(BF))))[0]
        x[r][:, s == 0] = u[r][:, None, :4].astype(np.float32)
        x[r][:, (s < 0) != wish[r]] *= -1
    return (x + np.float32(0)).reshape(N, 128, 4 * T).astype(BF)
def some(rng, n):
    return np.stack([rng.permutation(T) < n[r] for r in range(N)])
def setup_inputs(rng):
    return plain(rng)
def setup_inputs_many(rng):
    d = plain(rng)
    n = rng.integers(CAPP + 1, T + 1, N)
    j = 2 * int(rng.integers(0, N // 2))
    n[j:j + 2] = CAPP
    d["x"] = aim(d["x"], d["u"], some(rng, n))
    return d
def setup_inputs_none(rng):
    d = plain(rng)
    wish = some(rng, rng.integers(T // 4, T + 1, N))
    i, j = 2 * rng.permutation(N // 2)[:2] + rng.integers(0, 2, 2)
    wish[i] = False
    wish[i ^ 1] = True
    wish[j] = np.arange(T) == T - 1
    d["u"][int(rng.integers(0, N)), :, 4:8] = 0
    d["x"] = aim(d["x"], d["u"], wish)
    return d
def setup_inputs_zero(rng):
    d = plain(rng)
    d["u"][:, 64:, :4] = 0
    x = np.array(d["x"]).reshape(N, 128, T, 4)
    for r in range(N):
        e = rng.permutation(T)
        x[r][:, e[:T // 8]] = 0
        x[r][:64, e[T // 8:3 * T // 8]] = 0
    d["x"] = x.reshape(N, 128, 4 * T)
    return d
def setup_inputs_turn(rng):
    d = plain(rng)
    d["x"] = aim(d["x"], d["u"], some(rng, np.full(N, T // 2)))
    m, e = np.zeros((128, L, 4, 128, 4), np.float32), np.arange(128)
    for b in range(L):
        for i in range(4): m[e, b, i, e, i] = -16
    d["w"] = mx_ref.flush((m.reshape(128, 2048 * L) + d["w"].astype(np.float32) * np.float32(2.0 ** -6)).astype(BF))
    return d
def setup_inputs_spread(rng):
    d = plain(rng)
    u = np.array(wide(rng, N, 128, 512))
    u[:, :, 4 * L:] = 0
    return {**d, "x": wide(rng, N, 128, 4 * T, cols=6), "u": u, "v": wide(rng, N, 128, 512)}
def check_inputs(d):
    b = []
    for k in ("x", "u", "w", "v"):
        if not fit(d[k], 2.0 ** -30, 2.0 ** 30): b.append("a value of " + k)
    if (d["u"][:, :, 4 * L:].astype(np.float32) != 0).any(): b.append("u has numbers behind its first L columns")
    if not b:
        try:
            made = game(d["x"], d["u"], d["w"])[3]
            good, even = all(fit(t, 2.0 ** -60, 2.0 ** 60) for t in made), all(fit(blocks(t), 2.0 ** -30, 2.0 ** 30) for t in made)
        except Exception: good = even = False
        if not good: b.append("a number that an expert gives")
        if not even: b.append("the largest number of a block that an expert gives")
    return b
def reference(x, u, w, v):
    S, at, ks, made = game(x, u, w)
    oc, osc = np.zeros((N, 128, 4 * T), np.uint8), np.zeros((N, 16, T), np.uint8)
    y = np.zeros((N, 128, T), np.float32)
    for r in range(N):
        oc[r], osc[r] = emit(S[r])
        y[r] = mx_ref.matmul(mx_ref.quantize(np.ascontiguousarray(v[r])), S[r])
    return {"oc": oc, "osc": osc, "ids": at.reshape(N, 1, T).astype(np.float32), "ks": ks, "y": y}

@@ -1,0 +1,424 @@
+from concourse.mybir import dt, AluOpType, ActivationFunctionType
+
+L, CAPP, NP = 3, 48, 128
+WIN = NP + CAPP
+A = AluOpType
+F = ActivationFunctionType
+LOADS = {"x": [(0, 0, 2), (0, 2, 2), (1, 0, 4), (L, 0, 0)], "p0": [(2, 0, 4)]}
+ORDER = ("eeomoeooomgoemgmmmnnmn", "eeeeosmosomosmnosmmomnmonmvm", "eteeotoelmtlotolmomnmtomtmonmn")
+
+SCRATCH = {}
+
+
+def _mx(name, n):
+    SCRATCH["c" + name] = ("sbuf", [128, n], "float8_e4m3fn_x4")
+    SCRATCH["s" + name] = ("sbuf", [128, n], "uint8")
+
+
+def _sb(name, n, dtype="float32"):
+    SCRATCH[name] = ("sbuf", [128, n], dtype)
+
+
+for _b in range(L):
+    _mx("A%d" % _b, 128)
+    _mx("M%d" % _b, WIN)
+    _mx("X%d" % _b, WIN)
+    _mx("G%d" % _b, 128)
+    _mx("W%d" % _b, 512)
+    _sb("wt%d" % _b, 2048, "bfloat16")
+    _sb("gt%d" % _b, 512, "bfloat16")
+    _sb("ht%d" % _b, 512, "bfloat16")
+    _sb("wa%d" % _b, 128, "bfloat16")
+    _sb("cc%d" % _b, 128, "bfloat16")
+    _sb("wd%d" % _b, 128, "bfloat16")
+    _sb("yd%d" % _b, 128, "bfloat16")
+    _sb("dd%d" % _b, 128, "bfloat16")
+    _sb("jk%d" % _b, 384, "bfloat16")
+    _sb("su%d" % _b, 4)
+    _sb("sm%d" % _b, 64)
+    _sb("zz%d" % _b, 4, "uint16")
+    _sb("lo%d" % _b, 4, "uint16")
+    _sb("ml%d" % _b, 8, "uint16")
+    _sb("lz%d" % _b, 4, "uint16")
+    _sb("im%d" % _b, WIN)
+    _sb("iw%d" % _b, WIN)
+_mx("A3", 128)
+_mx("P0", 128)
+_mx("P1", 128)
+_mx("R", WIN)
+_mx("P2", 128)
+_mx("V", 128)
+_sb("xt", 512, "bfloat16")
+_sb("ut", 4 * L, "bfloat16")
+_sb("vt", 512, "bfloat16")
+_sb("zb", 128, "bfloat16")
+_sb("ia", 128, "int32")
+_sb("ib", 128, "int32")
+_sb("iq", 8, "int32")
+_sb("ir", 8, "int32")
+_sb("ic", 8)
+_sb("pj", 24)
+_sb("th", 128)
+_sb("r0", 128, "bfloat16")
+_sb("rm", 128, "bfloat16")
+_sb("cw", WIN)
+_sb("kj", CAPP * L)
+_sb("it", 256)
+_sb("pa", 8)
+_sb("px", 4, "uint16")
+_sb("pl", 4, "uint16")
+_sb("qx", 4, "uint16")
+_sb("ql", 4, "uint16")
+_sb("mx1", 4, "uint16")
+_sb("mxl", 4, "uint16")
+_sb("pm", 8, "uint16")
+_sb("ui", 16, "int32")
+_sb("uj", 16, "int32")
+_sb("ex", 256)
+_sb("idf", 128)
+_sb("kk", 12)
+_sb("yt", 128)
+SCRATCH["pe"] = ("psum", [128, 2048], "float32")
+SCRATCH["ps"] = ("psum", [128, 512], "float32")
+SCRATCH["py"] = ("psum", [128, 512], "float32")
+
+SEMAPHORES = (["vs", "ss", "ts", "gs", "gi", "sent", "dx", "du", "dv", "out", "dm0", "dm1"]
+              + ["dw%d%d" % (b, i) for b in range(L) for i in range(4)]
+              + ["ap0", "ap1", "ar0", "ar1", "az0", "az1", "az2", "ai1", "ai2", "aml"])
+
+
+def rank_program(g, core, T, topo):
+    rank = T.rank_of(core)
+    if rank is None:
+        return
+    peers = [T.cores[rank ^ (1 << b)] for b in range(L)]
+    queue = {"v": g.vector, "s": g.scalar, "t": g.tensor, "g": g, "y": g.sync}
+    total, known = {}, {q: {} for q in queue}
+
+    def need(q, deps):
+        for d in deps:
+            if d is None:
+                continue
+            s, n = d
+            if known[q].get(s, 0) < n:
+                queue[q].wait_ge(T.sem[s], n)
+                known[q][s] = n
+
+    def did(instr, s, n):
+        instr.then_inc(T.sem[s], n)
+        total[s] = total.get(s, 0) + n
+        return (s, total[s])
+
+    def V(call, *deps):
+        need("v", deps)
+        return did(call(g.vector), "vs", 1)
+
+    def S(call, *deps):
+        need("s", deps)
+        return did(call(g.scalar), "ss", 1)
+
+    def E(call, *deps):
+        need("t", deps)
+        return did(call(g.tensor), "ts", 1)
+
+    def I(call, *deps):
+        need("g", deps)
+        return did(call(g), "gs", 1)
+
+    def load(q, sem, out, in_, *deps):
+        need(q, deps)
+        return did(queue[q].dma_start(out, in_), sem, 16)
+
+    def mask(dst, quiet=False):
+        es = topo.engines(core, dst)
+        if quiet:
+            es = [e for e in es if e not in topo.engines(core, peers[2])] or es
+        m = 0
+        for e in es:
+            m |= 1 << e
+        return m, len(es)
+
+    def send(dst, out, in_, sem, *deps, quiet=False):
+        need("g", deps)
+        m, n = mask(dst, quiet)
+        rid, pid, _ = topo.addr(dst)
+        g.remote_dma(out, in_, T.sem[sem], T.sem["sent"], pid, rid, m)
+        total["sent"] = total.get("sent", 0) + n
+        total[sem] = total.get(sem, 0) + n
+        return (sem, total[sem])
+
+    def send_codes(dst, to, frm, a, b, sem, *deps):
+        return send(dst, T["c" + to][:, a:b].bitcast(dt.uint8), T["c" + frm][:, a:b].bitcast(dt.uint8), sem, *deps)
+
+    def send_scales(dst, to, frm, a, b, sem, *deps):
+        return send(dst, T["s" + to][:, a:b], T["s" + frm][:, a:b], sem, *deps)
+
+    def pick_c(to, a, b, frm, n, off, k, *deps):
+        return V(lambda q: q.tensor_copy(T["c" + to][:, a:b].bitcast(dt.uint32),
+                                         T["c" + frm][:, 0:n].bitcast(dt.uint32).indirect(T[off][:, 0:k])), *deps)
+
+    def pick_s(to, a, b, frm, n, off, k, *deps):
+        return S(lambda q: q.activation(T["s" + to][:, a:b], T["s" + frm][:, 0:n].indirect(T[off][:, 0:k]), F.Copy), *deps)
+
+    def pick_n(out, frm, n, off, k, *deps):
+        return S(lambda q: q.activation(out, T[frm][:, 0:n].indirect(T[off][:, 0:k]), F.Copy), *deps)
+
+    def quant(to, a, b, in_, *deps):
+        return V(lambda q: q.quantize_mx(T["c" + to][:, a:b], T["s" + to][:, a:b], in_), *deps)
+
+    dx = load("y", "dx", T.xt[:], T.x[:])
+    du = load("s", "du", T.ut[:], T.u[:, 0:4 * L])
+    dw = {b: {} for b in range(L + 1)}
+
+    def issued():
+        g.sem_inc(T.sem["gi"], 1)
+        total["gi"] = total.get("gi", 0) + 1
+        return ("gi", total["gi"])
+
+    def point(name, *deps):
+        for b, i, w in LOADS[name]:
+            if b == L:
+                dw[b][i, w] = load("y", "dv", T.vt[:], T.v[:], *deps)
+            else:
+                dw[b][i, w] = load("y", "dw%d%d" % (b, i), T["wt%d" % b][:, 512 * i:512 * i + 512 * w],
+                                   T.w[:, 2048 * b + 512 * i:2048 * b + 512 * i + 512 * w], *deps)
+
+    point("x")
+
+    zb = V(lambda q: q.memset(T.zb[:], 0.0))
+    zx = V(lambda q: q.memset(T.ex[:], 0.0))
+    c1 = V(lambda q: q.memset(T.cw[:, 0:NP], 1.0))
+    c2 = V(lambda q: q.memset(T.cw[:, NP:WIN], 0.0))
+    flag = {"allow_small_or_imprecise_dtypes": True}
+    iq = I(lambda q: q.iota(T.iq[:], [[0, 8]], 0, 1))
+    ic = I(lambda q: q.iota(T.ic[:], [[16, 8]], 0, 0, **flag))
+    ia = I(lambda q: q.iota(T.ia[:], [[1, 128]], 128, -1))
+    r0 = I(lambda q: q.iota(T.r0[:], [[0, 8], [1, 16]], 0, 0, **flag))
+    im = I(lambda q: q.iota(T.im0[:, 0:NP], [[1, NP]], rank * NP, 0, **flag))
+    iw = I(lambda q: q.iota(T.iw0[:, 0:NP], [[1, NP]], (rank ^ 1) * NP, 0, **flag))
+    p8, jb, jc = T.pj[:, 0:8], T.pj[:, 8:16], T.pj[:, 16:24]
+    ir = V(lambda q: q.tensor_scalar(T["ir"][:], T.iq[:], 15, None, A.bitwise_and), iq)
+    kp8 = V(lambda q: q.tensor_tensor(p8, T["ir"][:], T.ic[:], A.add), ir, ic)
+    kjb = V(lambda q: q.tensor_scalar(jb, p8, NP - 0.5, None, A.add), kp8)
+    kjc = V(lambda q: q.tensor_scalar(jc, p8, NP - 1.0, None, A.add), kp8)
+    ib = V(lambda q: q.tensor_scalar(T.ib[:], T.ia[:], 15, None, A.bitwise_and), ia)
+    th = V(lambda q: q.tensor_scalar(T.th[:], T.ib[:], 0.0, -1e29, A.not_equal, A.mult), ib)
+    rm = V(lambda q: q.tensor_scalar(T.rm[:], T.r0[:], 0.0, None, A.is_gt), r0)
+
+    def gauge(b):
+        return [S(lambda q: q.activation(T["gt%d" % b][:, t:512:4], T.zb[:], F.Identity, bias=T.ut[:, 4 * b + t:4 * b + t + 1]), zb, du)
+                for t in range(4)][-1]
+
+    gg = {0: gauge(0)}
+    Ac = As = quant("A0", 0, NP, T.xt[:], dx)
+    qg = {0: quant("G0", 0, NP, T.gt0[:], gg[0])}
+    Mc = Ms = quant("M0", 0, NP, T.xt[:], dx)
+
+    send_codes(peers[0], "P0", "A0", 0, NP, "ap0", Ac)
+    P = send_scales(peers[0], "P0", "A0", 0, NP, "ap0", As)
+
+    ids, idp = im, iw
+    k = {"wa": None, "wd": None, "ml": None}
+    casts, az, ccs, kp = [None] * 4, [], [], []
+
+    def turns(order, **chains):
+        for c in order:
+            next(chains[c], 0)
+        for c in chains:
+            for _ in chains[c]:
+                pass
+
+    def count(b):
+        kp.append(S(lambda q: q.activation(T.kj[:, CAPP * b:CAPP * b + CAPP], T.cw[:, 0:WIN].indirect(T["lz%d" % b][:, 0:3]), F.Copy,
+                                           accum_out=T.kk[:, b:b + 1]), c1, c2, az[b]))
+
+    def expert(b):
+        for i in range(4):
+            d = [t for (j, w), t in dw[b].items() if j <= i < j + w]
+            t = quant("W%d" % b, 128 * i, 128 * i + 128, T["wt%d" % b][:, 512 * i:512 * i + 512], *d)
+            if i == 3:
+                k["qw%d" % b] = t
+            yield 1
+
+    def side_v():
+        k["qv"] = quant("V", 0, NP, T.vt[:], *dw[L].values())
+        yield 1
+
+    def gauges():
+        for j in (1, 2):
+            gg[j] = gauge(j)
+        yield 1
+        qg[1] = quant("G1", 0, NP, T.gt1[:], gg[1])
+        yield 1
+
+    def own_list(b):
+        n = "%d" % b
+        sm, su, cc = T["sm" + n], T["su" + n], T["cc" + n]
+        k["wa"] = V(lambda q: q.tensor_scalar(T["wa" + n][:], T.ps[:, 0:NP], 0.0, None, A.is_lt), k["sc"])
+        yield 1
+        k["ct"] = V(lambda q: q.tensor_tensor_scan(cc[:], T["wa" + n][:], T["wa" + n][:], NP - 1.0, A.add, A.max), k["wa"])
+        ccs.append(k["ct"])
+        sums = [S(lambda q: q.activation(T["jk" + n][:, NP * c:NP * c + NP], cc[:], F.Sign, bias=T.pj[:, 8 + c:9 + c], scale=-1.0,
+                                         accum_out=su[:, c:c + 1]), k["ct"], kjb) for c in range(3)]
+        yield 1
+        for c in range(3):
+            t = V(lambda q: q.tensor_scalar(sm[:, c:c + 1], cc[:, NP - 1:NP], T.pj[:, 16 + c:17 + c], T.pj[:, c:c + 1], A.is_le, A.mult),
+                  k["ct"], kjc)
+        yield 1
+        t = V(lambda q: q.tensor_scalar(sm[:, 8:11], sm[:, 0:3], 64.0, None, A.add), t)
+        yield 1
+        for c in range(3):
+            z = V(lambda q: q.tensor_scalar(T["zz" + n][:, c:c + 1], su[:, c:c + 1], 0.5, sm[:, 8 + c:9 + c], A.mult, A.add), t, sums[c])
+        az.append(send(peers[b], T["lz" + n][:, 0:3], T["zz" + n][:, 0:3], "az" + n, z, quiet=(b == 1)))
+        yield 1
+        lo = k["lo"] = V(lambda q: q.tensor_scalar(T["lo" + n][:, 0:3], T["zz" + n][:, 0:3], float(NP - 1), None, A.min), z)
+        yield 1
+        k["xc"] = pick_c("X" + n, NP, WIN, "A" + n, NP, "lo" + n, 3, lo, Ac)
+        k["xs"] = pick_s("X" + n, NP, WIN, "A" + n, NP, "lo" + n, 3, lo, As)
+        yield 1
+
+    def merging_list(b):
+        n = "%d" % b
+        sm, cc = T["sm" + n], T["cc" + n]
+        k["wd"] = V(lambda q: q.tensor_tensor(T["wd" + n][:], T.ps[:, 0:NP], T.th[:], A.is_lt), k["sc"], th)
+        yield 1
+        t = V(lambda q: q.tensor_tensor(T["yd" + n][:], T["wd" + n][:], cc[:], A.mult), k["wd"], k["ct"])
+        yield 1
+        t = V(lambda q: q.tensor_tensor_scan(T["dd" + n][:], T.rm[:], T["yd" + n][:], 0.0, A.mult, A.add), t, rm)
+        yield 1
+        d8 = T["dd" + n][:, 15:128:16]
+        t = V(lambda q: q.tensor_scalar(sm[:, 16:24], d8, float(WIN - 1), None, A.is_le), t)
+        yield 1
+        t = V(lambda q: q.tensor_tensor(sm[:, 24:32], sm[:, 16:24], d8, A.mult), t)
+        yield 1
+        t = V(lambda q: q.tensor_tensor(sm[:, 32:40], sm[:, 24:32], T.pj[:, 0:8], A.max), t, kp8)
+        yield 1
+        k["ml"] = V(lambda q: q.tensor_copy(T["ml" + n][:], sm[:, 32:40]), t)
+        if b == 1:
+            t = V(lambda q: q.tensor_scalar(sm[:, 40:44], sm[:, 32:36], 256.0, None, A.mult), t)
+            yield 1
+            t = V(lambda q: q.tensor_tensor(sm[:, 44:48], sm[:, 40:44], sm[:, 36:40], A.add), t)
+            yield 1
+            t = V(lambda q: q.tensor_copy(T.mx1[:], sm[:, 44:48]), t)
+            k["aml"] = send(peers[2], T.mxl[:], T.mx1[:], "aml", t)
+        yield 1
+
+    def send_numbers():
+        base = float(NP * (rank & ~1))
+        t = V(lambda q: q.transpose(T.it[:, 0:NP], T.im1[:, 0:NP]), ids)
+        yield 1
+        t = V(lambda q: q.tensor_scalar(T.pa[:, 0:2], T.it[:, 0:64:32], 256.0, -257.0 * base, A.mult, A.add), t)
+        yield 1
+        t = V(lambda q: q.tensor_tensor(T.pa[:, 4:6], T.pa[:, 0:2], T.it[:, 64:128:32], A.add), t)
+        yield 1
+        t = V(lambda q: q.tensor_copy(T.px[:, 0:2], T.pa[:, 4:6]), t)
+        k["ai1"] = send(peers[1], T.pl[:, 0:2], T.px[:, 0:2], "ai1", t, quiet=True)
+        yield 1
+
+    def take_numbers():
+        base = float(NP * ((rank ^ 2) & ~1))
+        e = V(lambda q: q.tensor_copy(T.ui[:, 0:2], T.pl[:, 0:2]), k["ai1"])
+        yield 1
+        e1 = V(lambda q: q.tensor_scalar(T.uj[:, 0:2], T.ui[:, 0:2], 8, None, A.logical_shift_right), e)
+        e2 = V(lambda q: q.tensor_scalar(T.uj[:, 4:6], T.ui[:, 0:2], 255, None, A.bitwise_and), e)
+        yield 1
+        e1 = V(lambda q: q.tensor_scalar(T.ex[:, 0:64:32], T.uj[:, 0:2], base, None, A.add), e1, zx)
+        e2 = V(lambda q: q.tensor_scalar(T.ex[:, 64:128:32], T.uj[:, 4:6], base, None, A.add), e2)
+        yield 1
+        idp = V(lambda q: q.transpose(T.iw1[:, 0:NP], T.ex[:, 0:NP]), e1, e2)
+        idn = pick_n(T.im1[:, NP:WIN], "iw1", WIN, "lz1", 3, idp, idw, az[1])
+        k["ids"] = pick_n(T.im2[:, 0:NP], "im1", WIN, "ml1", 8, idn, ids, old)
+        yield 1
+        e = V(lambda q: q.transpose(T.it[:, NP:2 * NP], T.im2[:, 0:NP]), k["ids"])
+        yield 1
+        e = V(lambda q: q.tensor_copy(T.qx[:], T.it[:, NP:2 * NP:32]), e)
+        k["ai2"] = send(peers[2], T.ql[:], T.qx[:], "ai2", e)
+        yield 1
+
+    def take_list():
+        e = V(lambda q: q.tensor_copy(T.ui[:, 4:8], T.mxl[:]), k["aml"])
+        yield 1
+        e1 = V(lambda q: q.tensor_scalar(T.uj[:, 8:12], T.ui[:, 4:8], 8, None, A.logical_shift_right), e)
+        e2 = V(lambda q: q.tensor_scalar(T.uj[:, 12:16], T.ui[:, 4:8], 255, None, A.bitwise_and), e)
+        yield 1
+        e1 = V(lambda q: q.tensor_copy(T.pm[:, 0:4], T.uj[:, 8:12]), e1)
+        k["pm"] = V(lambda q: q.tensor_copy(T.pm[:, 4:8], T.uj[:, 12:16]), e2)
+        yield 1
+
+    def new_columns(b):
+        n = "%d" % b
+        h = T["ht" + n]
+        Pd = (P,)
+        if b == 2:
+            Pd = (pick_c("P2", 0, NP, "R", WIN, "pm", 8, k["pm"], ar0, ar1), pick_s("P2", 0, NP, "R", WIN, "pm", 8, k["pm"], ar0, ar1))
+        mm = [E(lambda q: q.matmul_mx(T.pe[:, 512 * i:512 * i + NP], T["cW" + n][:, 128 * i:128 * i + 128], T["sW" + n][:, 128 * i:128 * i + 128],
+                                      T["cP" + n][:, 0:NP], T["sP" + n][:, 0:NP], True, True), k["qw" + n], casts[i], *Pd) for i in range(4)]
+        for i in range(3):
+            casts[i] = S(lambda q: q.activation(h[:, i:512:4], T.pe[:, 512 * i:512 * i + NP], F.Copy, scale=0.0625), mm[i])
+        yield 1
+        casts[3] = V(lambda q: q.tensor_scalar(h[:, 3:512:4], T.pe[:, 1536:1536 + NP], 0.0625, None, A.mult), mm[3])
+        yield 1
+        k["qn"] = quant("X" + n, 0, NP, h[:], *casts)
+        yield 1
+
+    for b in range(L):
+        n = "%d" % b
+        if b == 1:
+            ids = pick_n(T.im1[:, 0:NP], "im0", WIN, "ml0", 8, idn, ids, k["ml"])
+        k["sc"] = E(lambda q: q.matmul_mx(T.ps[:, 0:NP], T["cG" + n][:, 0:NP], T["sG" + n][:, 0:NP], T["cA" + n][:, 0:NP],
+                                          T["sA" + n][:, 0:NP], True, True), qg[b], Ac, As, k["wa"], k["wd"])
+        old = k["ml"]
+        if b == 0:
+            turns(ORDER[0], o=own_list(0), m=merging_list(0), g=gauges(), e=expert(0), n=new_columns(0))
+            point("p0", P)
+            qg[2] = quant("G2", 0, NP, T.gt2[:], gg[2])
+        if b == 1:
+            turns(ORDER[1], e=expert(1), o=own_list(1), s=send_numbers(), m=merging_list(1), n=new_columns(1), v=side_v())
+            last = expert(2)
+            next(last)
+        if b == 2:
+            turns(ORDER[2], e=last, t=take_numbers(), o=own_list(2), l=take_list(), n=new_columns(2), m=merging_list(2))
+            ids, ai2 = k["ids"], k["ai2"]
+        idw = pick_n(T["iw" + n][:, NP:WIN], "im" + n, NP, "lo" + n, 3, k["lo"], ids)
+        if b == 0:
+            idn = pick_n(T.im0[:, NP:WIN], "iw0", WIN, "lz0", 3, idp, idw, az[0])
+        if b == 2:
+            for j in range(L):
+                count(j)
+        nc = pick_c("M" + n, NP, WIN, "X" + n, WIN, "lz" + n, 3, k["qn"], k["xc"], az[b])
+        ns = pick_s("M" + n, NP, WIN, "X" + n, WIN, "lz" + n, 3, k["qn"], k["xs"], az[b])
+        if b == 1:
+            send_codes(peers[2], "R", "M1", NP, WIN, "ar1", nc)
+            ar1 = send_scales(peers[2], "R", "M1", NP, WIN, "ar1", ns)
+        o = "%d" % (b + 1)
+        Ac = pick_c("A" + o, 0, NP, "M" + n, WIN, "ml" + n, 8, nc, k["ml"], Mc)
+        As = pick_s("A" + o, 0, NP, "M" + n, WIN, "ml" + n, 8, ns, k["ml"], Ms)
+        if b == 0:
+            send_codes(peers[1], "P1", "A1", 0, NP, "ap1", Ac)
+            P = send_scales(peers[1], "P1", "A1", 0, NP, "ap1", As)
+        if b < 2:
+            sent = issued()
+            load("y", "dm" + n, T["cM" + o][:, 0:NP].bitcast(dt.uint8), T["cA" + o][:, 0:NP].bitcast(dt.uint8), Ac, sent)
+            Mc = Ms = load("y", "dm" + n, T["sM" + o][:, 0:NP], T["sA" + o][:, 0:NP], As)
+        if b == 0:
+            send_codes(peers[2], "R", "A1", 0, NP, "ar0", Ac)
+            ar0 = send_scales(peers[2], "R", "A1", 0, NP, "ar0", As)
+
+    ym = E(lambda q: q.matmul_mx(T.py[:, 0:NP], T.cV[:, 0:NP], T.sV[:, 0:NP], T.cA3[:, 0:NP], T.sA3[:, 0:NP], True, True), k["qv"], Ac, As)
+    load("y", "out", T.oc[:, 0:4 * NP], T.cA3[:, 0:NP].bitcast(dt.uint8), Ac)
+    for j in range(4):
+        load("y", "out", T.osc[4 * j:4 * j + 4, 0:NP], T.sA3[32 * j:32 * j + 4, 0:NP], As)
+    kk = [V(lambda q: q.tensor_scalar(T.kk[:, 4 + b:5 + b], T.kk[:, b:b + 1], NP - 1.0, T["cc%d" % b][:, NP - 1:NP], A.add, A.min), kp[b], ccs[b])
+          for b in range(L)][-1]
+    e = V(lambda q: q.tensor_copy(T.ex[:, NP:2 * NP:32], T.ql[:]), ai2, zx)
+    kk = V(lambda q: q.tensor_scalar(T.kk[:, 8:8 + L], T.kk[:, 4:4 + L], 1.0 - NP, None, A.add), kk)
+    idp = V(lambda q: q.transpose(T.iw2[:, 0:NP], T.ex[:, NP:2 * NP]), e)
+    yt = V(lambda q: q.tensor_copy(T.yt[:], T.py[:, 0:NP]), ym)
+    load("y", "out", T.y[:], T.yt[:], yt)
+    load("y", "out", T.ks[:], T.kk[0:1, 8:8 + L], kk)
+    idn = pick_n(T.im2[:, NP:WIN], "iw2", WIN, "lz2", 3, idp, idw, az[2])
+    idf = pick_n(T.idf[:], "im2", WIN, "ml2", 8, idn, ids, k["ml"])
+    load("y", "out", T.ids[:], T.idf[0:1, :], idf)
+
+    for s in sorted(total):
+        need("g", [(s, total[s])])

@@ -2,10 +2,16 @@ from concourse.mybir import dt, AluOpType, ActivationFunctionType
 
 L, CAPP, NP = 3, 48, 128
 WIN = NP + CAPP
+SEG = NP + 1
+CUT = 88
+LOW = 2048.0
 A = AluOpType
 F = ActivationFunctionType
-LOADS = {"x": [(0, 0, 2), (0, 2, 2), (1, 0, 4), (L, 0, 0)], "p0": [(2, 0, 4)]}
-ORDER = ("eeomoeooomgoemgmmmnnmn", "eeeeosmosomosmnosmmomnmonmvm", "eteeotoelmtlotolmomnmtomtmonmn")
+LOADS = [(0, 0, 2, None), (0, 2, 2, None), (1, 0, 4, None), (3, 0, 1, None), (2, 0, 4, "ap0s")]
+CASTS = "svsvsvsvsvsvv"
+OUTS = "yyyyssyy"
+AGAIN = ("nw0", "nw1", "nw2")
+ORDER = [10, 1, 6, 0, 9, 7, 2, 3, 15, 4, 8, 16, 29, 13, 11, 18, 17, 27, 35, 12, 20, 19, 36, 14, 38, 37, 32, 39, 31, 48, 43, 49, 40, 23, 53, 22, 41, 55, 72, 21, 25, 34, 52, 56, 30, 24, 42, 74, 28, 44, 59, 57, 47, 58, 26, 46, 63, 33, 60, 45, 71, 73, 61, 64, 125, 50, 62, 67, 68, 66, 65, 77, 54, 76, 5, 75, 78, 81, 80, 79, 82, 88, 69, 90, 83, 70, 84, 85, 51, 86, 87, 126, 89, 127, 91, 98, 124, 99, 92, 96, 102, 112, 101, 93, 100, 111, 97, 170, 103, 94, 167, 104, 171, 117, 129, 105, 128, 130, 131, 133, 132, 121, 95, 134, 120, 135, 113, 119, 118, 122, 136, 169, 123, 137, 138, 106, 141, 139, 142, 107, 145, 110, 109, 140, 108, 168, 148, 143, 149, 144, 159, 114, 158, 150, 152, 151, 115, 146, 153, 116, 147, 154, 155, 172, 160, 164, 173, 192, 163, 161, 162, 165, 174, 175, 176, 177, 178, 179, 180, 181, 166, 189, 182, 156, 183, 184, 193, 157, 185, 186, 194, 187, 195, 198, 190, 196, 199, 197, 191, 188, 200, 201]
 
 SCRATCH = {}
 
@@ -20,405 +26,342 @@ def _sb(name, n, dtype="float32"):
 
 
 for _b in range(L):
-    _mx("A%d" % _b, 128)
+    _mx("A%d" % _b, NP)
     _mx("M%d" % _b, WIN)
     _mx("X%d" % _b, WIN)
-    _mx("G%d" % _b, 128)
+    _mx("G%d" % _b, NP)
     _mx("W%d" % _b, 512)
+    _mx("P%d" % _b, NP)
     _sb("wt%d" % _b, 2048, "bfloat16")
     _sb("gt%d" % _b, 512, "bfloat16")
     _sb("ht%d" % _b, 512, "bfloat16")
-    _sb("wa%d" % _b, 128, "bfloat16")
-    _sb("cc%d" % _b, 128, "bfloat16")
-    _sb("wd%d" % _b, 128, "bfloat16")
-    _sb("yd%d" % _b, 128, "bfloat16")
-    _sb("dd%d" % _b, 128, "bfloat16")
-    _sb("jk%d" % _b, 384, "bfloat16")
-    _sb("su%d" % _b, 4)
-    _sb("sm%d" % _b, 64)
-    _sb("zz%d" % _b, 4, "uint16")
+    _sb("nw%d" % _b, NP, "bfloat16")
+    _sb("co%d" % _b, 3 * SEG, "bfloat16")
+    _sb("zz%d" % _b, 8, "uint16")
     _sb("lo%d" % _b, 4, "uint16")
-    _sb("ml%d" % _b, 8, "uint16")
-    _sb("lz%d" % _b, 4, "uint16")
+    _sb("lz%d" % _b, 8, "uint16")
     _sb("im%d" % _b, WIN)
     _sb("iw%d" % _b, WIN)
-_mx("A3", 128)
-_mx("P0", 128)
-_mx("P1", 128)
+for _b in range(L + 1):
+    _sb("mr%d" % _b, WIN, "bfloat16")
+    _sb("me%d" % _b, NP, "bfloat16")
+    _sb("ml%d" % _b, 8, "uint16")
+_mx("A3", NP)
 _mx("R", WIN)
-_mx("P2", 128)
-_mx("V", 128)
+_mx("H", NP)
+_mx("V", NP)
 _sb("xt", 512, "bfloat16")
 _sb("ut", 4 * L, "bfloat16")
 _sb("vt", 512, "bfloat16")
-_sb("zb", 128, "bfloat16")
-_sb("ia", 128, "int32")
-_sb("ib", 128, "int32")
-_sb("iq", 8, "int32")
-_sb("ir", 8, "int32")
-_sb("ic", 8)
-_sb("pj", 24)
-_sb("th", 128)
-_sb("r0", 128, "bfloat16")
-_sb("rm", 128, "bfloat16")
-_sb("cw", WIN)
-_sb("kj", CAPP * L)
-_sb("it", 256)
-_sb("pa", 8)
-_sb("px", 4, "uint16")
-_sb("pl", 4, "uint16")
-_sb("qx", 4, "uint16")
-_sb("ql", 4, "uint16")
-_sb("mx1", 4, "uint16")
-_sb("mxl", 4, "uint16")
-_sb("pm", 8, "uint16")
-_sb("ui", 16, "int32")
-_sb("uj", 16, "int32")
-_sb("ex", 256)
-_sb("idf", 128)
+_sb("zb", SEG, "bfloat16")
+_sb("tc", WIN, "bfloat16")
+_sb("ct", 3 * SEG, "bfloat16")
+_sb("dd", 3 * L * SEG, "bfloat16")
+_sb("ia", NP, "int32")
+_sb("ib", NP, "int32")
+_sb("iq", 4, "int32")
+_sb("cs", 8)
+_sb("k16", 3 * NP, "bfloat16")
+_sb("k128", 2 * SEG, "bfloat16")
+_sb("cw", WIN, "bfloat16")
+_sb("kj", CAPP * L, "bfloat16")
+_sb("ie", SEG)
+_sb("it", NP)
+_sb("ex", NP)
+_sb("lp", 4, "uint16")
+_sb("e1", 32)
+_sb("idf", NP)
 _sb("kk", 12)
-_sb("yt", 128)
+_sb("yt", NP)
 SCRATCH["pe"] = ("psum", [128, 2048], "float32")
 SCRATCH["ps"] = ("psum", [128, 512], "float32")
 SCRATCH["py"] = ("psum", [128, 512], "float32")
 
-SEMAPHORES = (["vs", "ss", "ts", "gs", "gi", "sent", "dx", "du", "dv", "out", "dm0", "dm1"]
-              + ["dw%d%d" % (b, i) for b in range(L) for i in range(4)]
-              + ["ap0", "ap1", "ar0", "ar1", "az0", "az1", "az2", "ai1", "ai2", "aml"])
+SEMAPHORES = (["v", "s", "t", "g", "sent", "out", "dx", "du"] + ["dw%d" % i for i in range(len(LOADS))]
+              + ["dm%d%s" % (b, c) for b in range(1, L) for c in "cs"] + ["ap%d%s" % (b, c) for b in range(L - 1) for c in "cs"]
+              + ["ahc", "ahs", "hrc", "hrs", "arc", "anc", "ans", "az0", "az1", "az2", "alp"])
+
+
+def helper(c, T, topo):
+    mine = [e for e in T.cores if topo.chip(e) == topo.chip(c)]
+    free = [e for e in topo.cores_of(c) if topo.die(e) != topo.die(c) and e not in T.cores]
+    return free[mine.index(c)]
+
+
+def engines(src, dst, far, quiet, topo):
+    return [e for e in topo.engines(src, dst) if not quiet or e not in topo.engines(src, far)]
+
+
+def bits(es):
+    return sum(1 << e for e in es)
+
+
+def build(core, T, topo):
+    rank = T.rank_of(core)
+    peers = [T.cores[rank ^ (1 << b)] for b in range(L)]
+    ops, seen, named = [], {}, {}
+
+    def p(name, a=0, b=None, step=1, off=None):
+        return (name, a, T[name].shape[1] if b is None else b, step, off)
+
+    def by(name, n, off, k):
+        return p(name, 0, n, 1, p(off, 0, k))
+
+    def view(x, word=None):
+        if not isinstance(x, tuple):
+            return x
+        v = T[x[0]][:, x[1]:x[2]:x[3]] if x[3] > 1 else T[x[0]][:, x[1]:x[2]]
+        if word is not None and SCRATCH[x[0]][2] == "float8_e4m3fn_x4":
+            v = v.bitcast(word)
+        return v if x[4] is None else v.indirect(view(x[4]))
+
+    def op(q, call, outs, ins, sem=None, n=1, name=None, after=(), more=None):
+        me, need = len(ops), set(named[a] for a in after if a is not None)
+        ins = [x for x in ins if isinstance(x, tuple)]
+        ins += [x[4] for x in outs + ins if x[4] is not None]
+        for xs, w in ((ins, False), (outs, True)):
+            for x in xs:
+                bank = SCRATCH[x[0]][0] == "psum"
+                cols = set(range(x[1] // 512 * 512, x[1] // 512 * 512 + 512) if bank else range(x[1], x[2], x[3]))
+                for j, c2, w2 in seen.setdefault(x[0], []):
+                    if j != me and (w or w2 or (bank and ops[j]["q"] != q)) and cols & c2:
+                        need.add(j)
+                seen[x[0]].append((me, cols, w))
+        ops.append({"q": q, "call": call, "need": need, "sem": sem or q, "n": n, "name": name, "more": more})
+        name = name or outs[0][0]
+        if name not in named:
+            named[name] = me
+            loads(name)
+
+    def ts(out, in0, s1, s2, *alu):
+        op("v", lambda e: e.tensor_scalar(view(out), view(in0), view(s1), view(s2), *alu), [out], [in0, s1, s2])
+
+    def tt(out, in0, in1, alu):
+        op("v", lambda e: e.tensor_tensor(view(out), view(in0), view(in1), alu), [out], [in0, in1])
+
+    def scan(out, d0, d1, init, op0, op1):
+        op("v", lambda e: e.tensor_tensor_scan(view(out), view(d0), view(d1), view(init), op0, op1), [out], [d0, d1, init])
+
+    def copy(out, in_):
+        op("v", lambda e: e.tensor_copy(view(out, dt.uint32), view(in_, dt.uint32)), [out], [in_])
+
+    def fill(out, c):
+        op("v", lambda e: e.memset(view(out), c), [out], [])
+
+    def turn(out, in_):
+        op("v", lambda e: e.transpose(view(out), view(in_)), [out], [in_])
+
+    def quant(to, a, b, in_):
+        c, s = p("c" + to, a, b), p("s" + to, a, b)
+        op("v", lambda e: e.quantize_mx(view(c), view(s), view(in_)), [c, s], [in_])
+
+    def act(out, in_, func=F.Copy, **kw):
+        op("s", lambda e: e.activation(view(out), view(in_), func, **{a: view(x) for a, x in kw.items()}),
+           [out] + [x for a, x in kw.items() if a == "accum_out"], [in_] + [x for a, x in kw.items() if a != "accum_out"])
+
+    def iota(out, pattern, base, mult, **kw):
+        op("g", lambda e: e.iota(view(out), pattern, base, mult, **kw), [out], [])
+
+    def choose(out, in_, value, base):
+        op("g", lambda e: e.affine_select(view(out), view(in_), [[1, SEG]], A.not_equal, value, base, -1), [out], [in_])
+
+    def product(out, w, a, x):
+        ins = [p("c" + w, a, a + NP), p("s" + w, a, a + NP), p("c" + x, 0, NP), p("s" + x, 0, NP)]
+        op("t", lambda e: e.matmul_mx(view(out), *[view(i) for i in ins], True, True), [out], ins)
+
+    def dma(q, sem, out, in_, outs, ins, after=()):
+        op(q, lambda e: e.dma_start(out, in_), outs, ins, sem=sem, n=16, name=sem, after=after)
+
+    def send(dst, out, in_, sem, quiet=False):
+        es = engines(core, dst, peers[2], quiet, topo)
+        rid, pid, _ = topo.addr(dst)
+        op("g", lambda e: e.remote_dma(view(out, dt.uint8), view(in_, dt.uint8), T.sem[sem], T.sem["sent"], pid, rid, bits(es)),
+           [out], [in_], sem=sem, n=len(es), name=sem, more={"sent": len(es)})
+
+    def send_by_helper(k, a):
+        hc = helper(core, T, topo)
+        es = engines(core, hc, peers[2], k == "s", topo)
+        rid, pid, _ = topo.addr(hc)
+        op("g", lambda e: e.remote_dma(view(p(k + "H", a, NP), dt.uint8), view(p(k + "A1", a, NP), dt.uint8), T.sem["ah" + k], T.sem["sent"], pid, rid, bits(es)),
+           [p(k + "R", a, NP)], [p(k + "A1", a, NP)], sem="hr" + k, n=len(topo.engines(hc, peers[2])), name="hr" + k, more={"sent": len(es)})
+
+    def pick(to, a, b, frm, n, off):
+        copy(p("c" + to, a, b), by("c" + frm, n, off, (b - a) // 16))
+        act(p("s" + to, a, b), by("s" + frm, n, off, (b - a) // 16))
+
+    def again(b):
+        for c in "cs":
+            o, i = p(c + "M%d" % b, 0, NP), p(c + "A%d" % b)
+            dma("y", "dm%d%s" % (b, c), view(o, dt.uint8), view(i, dt.uint8), [o], [i], [AGAIN[b]])
+
+    def merging(b, off):
+        n = "%d" % b
+        copy(by("mr" + n, WIN, off, 3), p("tc", NP, WIN))
+        scan(p("me" + n), p("k16", 0, NP), p("mr" + n, 0, NP), 0.0, A.add, A.min)
+        ts(p("ml" + n), p("me" + n, 15, NP, 16), p("cs", 1, 2), None, A.add)
+
+    def loads(name):
+        for i, (b, j, w, after) in enumerate(LOADS):
+            if after != name:
+                continue
+            if b == L:
+                dma("y", "dw%d" % i, T.vt[:], T.v[:], [p("vt")], [], [after])
+            else:
+                o = p("wt%d" % b, 512 * j, 512 * (j + w))
+                dma("y", "dw%d" % i, view(o), T.w[:, 2048 * b + 512 * j:2048 * b + 512 * (j + w)], [o], [], [after])
+
+    dma("y", "dx", T.xt[:], T.x[:], [p("xt")], [])
+    dma("s", "du", T.ut[:], T.u[:, 0:4 * L], [p("ut")], [])
+    loads(None)
+    flag = {"allow_small_or_imprecise_dtypes": True}
+    iota(p("iq", 0, 2), [[0, 2]], 0, 1)
+    iota(p("tc"), [[1, WIN]], 0, 0, **flag)
+    iota(p("ia"), [[1, NP]], NP, -1)
+    fill(p("zb"), 0.0)
+    fill(p("dd", NP, None, SEG), -1.0)
+    act(p("ex"), p("tc", 0, NP), scale=0.0)
+    act(p("iw1", 0, NP), p("tc", 0, NP), scale=0.0)
+    act(p("e1"), p("tc", 0, 32), scale=0.0)
+    act(p("im1", NP, WIN), p("tc", 0, CAPP), scale=0.0)
+    ts(p("iq", 2, 3), p("iq", 0, 1), 15, None, A.bitwise_and)
+    ts(p("cs", 0, 1), p("iq", 2, 3), 1.0, None, A.add)
+    ts(p("cs", 1, 2), p("cs", 0, 1), 16.0, 256.0, A.is_lt, A.mult)
+    ts(p("cs", 4, 7), p("tc", 0, CAPP, 16), p("cs", 0, 1), None, A.add)
+    for c in range(3):
+        act(p("ct", SEG * c, SEG * c + NP), p("tc", 0, NP), scale=1.0 / 256)
+    ts(p("ct", NP, None, SEG), p("cs", 4, 7), NP - 1.0, 1.0 / 256, A.add, A.mult)
+    ts(p("ib"), p("ia", 0, NP), 15, None, A.bitwise_and)
+    ts(p("k16", NP, 2 * NP), p("ib"), 0.0, 1024.0, A.is_equal, A.mult)
+    ts(p("k16", 2 * NP, 3 * NP), p("ib"), 1.0, -256.0, A.is_equal, A.mult)
+    tt(p("k16", 0, NP), p("k16", NP, 2 * NP), p("k16", 2 * NP, 3 * NP), A.add)
+    choose(p("k128", SEG, 2 * SEG), p("zb", 0, SEG), 4 * LOW, 0)
+    choose(p("k128", 0, SEG), p("k128", SEG, 2 * SEG), -LOW, -1)
+    ts(p("cw"), p("tc"), float(NP), None, A.is_lt)
+    for b in range(L + 1):
+        act(p("mr%d" % b), p("tc"))
+    act(p("im0", 0, NP), p("tc", 0, NP), F.Identity, bias=float(rank * NP))
+    act(p("iw0", 0, NP), p("tc", 0, NP), F.Identity, bias=float((rank ^ 1) * NP))
+    for t in range(4):
+        ts(p("gt0", t, 512, 4), p("zb", 0, NP), p("ut", t, t + 1), None, A.add)
+    for b in (1, 2):
+        for t in range(4):
+            act(p("gt%d" % b, t, 512, 4), p("zb", 0, NP), F.Identity, bias=p("ut", 4 * b + t, 4 * b + t + 1))
+    quant("A0", 0, NP, p("xt"))
+    for b in range(L):
+        quant("G%d" % b, 0, NP, p("gt%d" % b))
+
+    for b in range(L):
+        n, o = "%d" % b, "%d" % (b + 1)
+        if b < 2:
+            for c in "cs":
+                send(peers[b], p(c + "P" + n), p(c + "A" + n), "ap" + n + c)
+        if b == 1:
+            send_by_helper("c", CUT)
+            send(peers[2], p("cR", 0, CUT), p("cA1", 0, CUT), "arc")
+            send_by_helper("s", 0)
+            scan(p("ie"), p("k128", 0, SEG), p("im1", 0, SEG), 0.0, A.add, A.min)
+            ts(p("zz1", 3, 4), p("ie", NP, SEG), LOW, None, A.add)
+        if b == 2:
+            turn(p("it"), p("im2", 0, NP))
+            copy(p("zz2", 3, 7), p("it", 0, NP, 32))
+        product(p("ps", 0, NP), "G" + n, 0, "A" + n)
+        ts(p("nw" + n), p("ps", 0, NP), 0.0, -1.0, A.is_lt, A.mult)
+        d = 3 * SEG * b
+        for c in range(3):
+            scan(p("dd", d + SEG * c, d + SEG * c + NP), p("nw" + n), p("zb", 0, NP), p("cs", 4 + c, 5 + c), A.add, A.add)
+        scan(p("co" + n), p("ct"), p("dd", d, d + 3 * SEG), 1.0, A.min, A.max)
+        ts(p("zz" + n, 0, 3), p("co" + n, NP, None, SEG), 256.0, None, A.mult)
+        send(peers[b], p("lz" + n, 0, (3, 4, 7)[b]), p("zz" + n, 0, (3, 4, 7)[b]), "az" + n, b == 1)
+        if b == 1:
+            copy(p("e1", 0, 1), p("lz1", 3, 4))
+            for a in range(0, NP, 32):
+                op("v", lambda e, a=a: e.transpose(T.iw1[0:32, a:a + 32], T.e1[a:a + 32, 0:32]), [p("iw1", a, a + 32)], [p("e1")])
+        if b == 2:
+            copy(p("ex", 0, NP, 32), p("lz2", 3, 7))
+            turn(p("iw2", 0, NP), p("ex"))
+        if b:
+            again(b)
+        else:
+            quant("M0", 0, NP, p("xt"))
+        if b == 1:
+            send(peers[2], p("lp", 0, 3), p("zz1", 0, 3), "alp")
+            merging(L, "lp")
+        ts(p("lo" + n, 0, 3), p("co" + n, NP, None, SEG), 256.0, NP - 1.0, A.mult, A.min)
+        pick("X" + n, NP, WIN, "A" + n, NP, "lo" + n)
+        act(p("iw" + n, NP, WIN), by("im" + n, NP, "lo" + n, 3))
+        merging(b, "zz" + n)
+        for i in range(4):
+            quant("W" + n, NP * i, NP * i + NP, p("wt" + n, 512 * i, 512 * i + 512))
+        if b == 2:
+            quant("V", 0, NP, p("vt"))
+            pick("P2", 0, NP, "R", WIN, "ml3")
+        for i in range(4):
+            product(p("pe", 512 * i, 512 * i + NP), "W" + n, NP * i, "P" + n)
+        for i in range(4):
+            h, r = p("ht" + n, i, 512, 4), p("pe", 512 * i, 512 * i + NP)
+            if CASTS[4 * b + i] == "v":
+                ts(h, r, 0.0625, None, A.mult)
+            else:
+                act(h, r, scale=0.0625)
+        quant("X" + n, 0, NP, p("ht" + n))
+        pick("M" + n, NP, WIN, "X" + n, WIN, "lz" + n)
+        if b == 1:
+            for c in "cs":
+                send(peers[2], p(c + "R", NP, WIN), p(c + "M1", NP, WIN), "an" + c)
+        pick("A" + o, 0, NP, "M" + n, WIN, "ml" + n)
+        act(p("im" + n, NP, WIN), by("iw" + n, WIN, "lz" + n, 3))
+        act(p("im" + o, 0, NP) if b < 2 else p("idf"), by("im" + n, WIN, "ml" + n, 8))
+        act(p("kj", CAPP * b, CAPP * b + CAPP), by("cw", WIN, "lz" + n, 3), accum_out=p("kk", b, b + 1))
+
+    product(p("py", 0, NP), "V", 0, "A3")
+    (copy if CASTS[4 * L] == "v" else act)(p("yt"), p("py", 0, NP))
+    ts(p("kk", 4, 4 + L), p("dd", NP - 1, None, 3 * SEG), -1.0, 1.0, A.mult, A.add)
+    tt(p("kk", 8, 8 + L), p("kk", 4, 4 + L), p("kk", 0, L), A.min)
+    dma(OUTS[0], "out", T.ks[:], T.kk[0:1, 8:8 + L], [], [p("kk", 8, 8 + L)])
+    dma(OUTS[1], "out", T.oc[:, 0:4 * NP], view(p("cA3"), dt.uint8), [], [p("cA3")])
+    for j in range(4):
+        dma(OUTS[2 + j], "out", T.osc[4 * j:4 * j + 4, 0:NP], T.sA3[32 * j:32 * j + 4, 0:NP], [], [p("sA3")])
+    dma(OUTS[6], "out", T.y[:], T.yt[:], [], [p("yt")])
+    dma(OUTS[7], "out", T.ids[:], T.idf[0:1, :], [], [p("idf")])
+    return ops
 
 
 def rank_program(g, core, T, topo):
-    rank = T.rank_of(core)
-    if rank is None:
+    if T.rank_of(core) is None:
+        for r, c in enumerate(T.cores):
+            if helper(c, T, topo) == core:
+                dst = T.cores[r ^ (1 << (L - 1))]
+                rid, pid, _ = topo.addr(dst)
+                off = topo.engines(core, dst)
+                g.wait_ge(T.sem["ahc"], len(engines(c, core, dst, False, topo)))
+                g.remote_dma(T.cR[:, CUT:NP].bitcast(dt.uint8), T.cH[:, CUT:NP].bitcast(dt.uint8), T.sem["hrc"], T.sem["sent"], pid, rid, bits(off))
+                g.wait_ge(T.sem["ahs"], len(engines(c, core, dst, True, topo)))
+                g.remote_dma(T.sR[:, 0:NP], T.sH[:, 0:NP], T.sem["hrs"], T.sem["sent"], pid, rid, bits(off))
+                g.wait_ge(T.sem["sent"], 2 * len(off))
         return
-    peers = [T.cores[rank ^ (1 << b)] for b in range(L)]
+    ops = build(core, T, topo)
     queue = {"v": g.vector, "s": g.scalar, "t": g.tensor, "g": g, "y": g.sync}
-    total, known = {}, {q: {} for q in queue}
+    total, known, done = {}, {q: {} for q in queue}, {}
 
-    def need(q, deps):
-        for d in deps:
-            if d is None:
-                continue
-            s, n = d
-            if known[q].get(s, 0) < n:
-                queue[q].wait_ge(T.sem[s], n)
-                known[q][s] = n
+    def wait(q, s, n):
+        if known[q].get(s, 0) < n:
+            queue[q].wait_ge(T.sem[s], n)
+            known[q][s] = n
 
-    def did(instr, s, n):
-        instr.then_inc(T.sem[s], n)
-        total[s] = total.get(s, 0) + n
-        return (s, total[s])
-
-    def V(call, *deps):
-        need("v", deps)
-        return did(call(g.vector), "vs", 1)
-
-    def S(call, *deps):
-        need("s", deps)
-        return did(call(g.scalar), "ss", 1)
-
-    def E(call, *deps):
-        need("t", deps)
-        return did(call(g.tensor), "ts", 1)
-
-    def I(call, *deps):
-        need("g", deps)
-        return did(call(g), "gs", 1)
-
-    def load(q, sem, out, in_, *deps):
-        need(q, deps)
-        return did(queue[q].dma_start(out, in_), sem, 16)
-
-    def mask(dst, quiet=False):
-        es = topo.engines(core, dst)
-        if quiet:
-            es = [e for e in es if e not in topo.engines(core, peers[2])] or es
-        m = 0
-        for e in es:
-            m |= 1 << e
-        return m, len(es)
-
-    def send(dst, out, in_, sem, *deps, quiet=False):
-        need("g", deps)
-        m, n = mask(dst, quiet)
-        rid, pid, _ = topo.addr(dst)
-        g.remote_dma(out, in_, T.sem[sem], T.sem["sent"], pid, rid, m)
-        total["sent"] = total.get("sent", 0) + n
-        total[sem] = total.get(sem, 0) + n
-        return (sem, total[sem])
-
-    def send_codes(dst, to, frm, a, b, sem, *deps):
-        return send(dst, T["c" + to][:, a:b].bitcast(dt.uint8), T["c" + frm][:, a:b].bitcast(dt.uint8), sem, *deps)
-
-    def send_scales(dst, to, frm, a, b, sem, *deps):
-        return send(dst, T["s" + to][:, a:b], T["s" + frm][:, a:b], sem, *deps)
-
-    def pick_c(to, a, b, frm, n, off, k, *deps):
-        return V(lambda q: q.tensor_copy(T["c" + to][:, a:b].bitcast(dt.uint32),
-                                         T["c" + frm][:, 0:n].bitcast(dt.uint32).indirect(T[off][:, 0:k])), *deps)
-
-    def pick_s(to, a, b, frm, n, off, k, *deps):
-        return S(lambda q: q.activation(T["s" + to][:, a:b], T["s" + frm][:, 0:n].indirect(T[off][:, 0:k]), F.Copy), *deps)
-
-    def pick_n(out, frm, n, off, k, *deps):
-        return S(lambda q: q.activation(out, T[frm][:, 0:n].indirect(T[off][:, 0:k]), F.Copy), *deps)
-
-    def quant(to, a, b, in_, *deps):
-        return V(lambda q: q.quantize_mx(T["c" + to][:, a:b], T["s" + to][:, a:b], in_), *deps)
-
-    dx = load("y", "dx", T.xt[:], T.x[:])
-    du = load("s", "du", T.ut[:], T.u[:, 0:4 * L])
-    dw = {b: {} for b in range(L + 1)}
-
-    def issued():
-        g.sem_inc(T.sem["gi"], 1)
-        total["gi"] = total.get("gi", 0) + 1
-        return ("gi", total["gi"])
-
-    def point(name, *deps):
-        for b, i, w in LOADS[name]:
-            if b == L:
-                dw[b][i, w] = load("y", "dv", T.vt[:], T.v[:], *deps)
-            else:
-                dw[b][i, w] = load("y", "dw%d%d" % (b, i), T["wt%d" % b][:, 512 * i:512 * i + 512 * w],
-                                   T.w[:, 2048 * b + 512 * i:2048 * b + 512 * i + 512 * w], *deps)
-
-    point("x")
-
-    zb = V(lambda q: q.memset(T.zb[:], 0.0))
-    zx = V(lambda q: q.memset(T.ex[:], 0.0))
-    c1 = V(lambda q: q.memset(T.cw[:, 0:NP], 1.0))
-    c2 = V(lambda q: q.memset(T.cw[:, NP:WIN], 0.0))
-    flag = {"allow_small_or_imprecise_dtypes": True}
-    iq = I(lambda q: q.iota(T.iq[:], [[0, 8]], 0, 1))
-    ic = I(lambda q: q.iota(T.ic[:], [[16, 8]], 0, 0, **flag))
-    ia = I(lambda q: q.iota(T.ia[:], [[1, 128]], 128, -1))
-    r0 = I(lambda q: q.iota(T.r0[:], [[0, 8], [1, 16]], 0, 0, **flag))
-    im = I(lambda q: q.iota(T.im0[:, 0:NP], [[1, NP]], rank * NP, 0, **flag))
-    iw = I(lambda q: q.iota(T.iw0[:, 0:NP], [[1, NP]], (rank ^ 1) * NP, 0, **flag))
-    p8, jb, jc = T.pj[:, 0:8], T.pj[:, 8:16], T.pj[:, 16:24]
-    ir = V(lambda q: q.tensor_scalar(T["ir"][:], T.iq[:], 15, None, A.bitwise_and), iq)
-    kp8 = V(lambda q: q.tensor_tensor(p8, T["ir"][:], T.ic[:], A.add), ir, ic)
-    kjb = V(lambda q: q.tensor_scalar(jb, p8, NP - 0.5, None, A.add), kp8)
-    kjc = V(lambda q: q.tensor_scalar(jc, p8, NP - 1.0, None, A.add), kp8)
-    ib = V(lambda q: q.tensor_scalar(T.ib[:], T.ia[:], 15, None, A.bitwise_and), ia)
-    th = V(lambda q: q.tensor_scalar(T.th[:], T.ib[:], 0.0, -1e29, A.not_equal, A.mult), ib)
-    rm = V(lambda q: q.tensor_scalar(T.rm[:], T.r0[:], 0.0, None, A.is_gt), r0)
-
-    def gauge(b):
-        return [S(lambda q: q.activation(T["gt%d" % b][:, t:512:4], T.zb[:], F.Identity, bias=T.ut[:, 4 * b + t:4 * b + t + 1]), zb, du)
-                for t in range(4)][-1]
-
-    gg = {0: gauge(0)}
-    Ac = As = quant("A0", 0, NP, T.xt[:], dx)
-    qg = {0: quant("G0", 0, NP, T.gt0[:], gg[0])}
-    Mc = Ms = quant("M0", 0, NP, T.xt[:], dx)
-
-    send_codes(peers[0], "P0", "A0", 0, NP, "ap0", Ac)
-    P = send_scales(peers[0], "P0", "A0", 0, NP, "ap0", As)
-
-    ids, idp = im, iw
-    k = {"wa": None, "wd": None, "ml": None}
-    casts, az, ccs, kp = [None] * 4, [], [], []
-
-    def turns(order, **chains):
-        for c in order:
-            next(chains[c], 0)
-        for c in chains:
-            for _ in chains[c]:
-                pass
-
-    def count(b):
-        kp.append(S(lambda q: q.activation(T.kj[:, CAPP * b:CAPP * b + CAPP], T.cw[:, 0:WIN].indirect(T["lz%d" % b][:, 0:3]), F.Copy,
-                                           accum_out=T.kk[:, b:b + 1]), c1, c2, az[b]))
-
-    def expert(b):
-        for i in range(4):
-            d = [t for (j, w), t in dw[b].items() if j <= i < j + w]
-            t = quant("W%d" % b, 128 * i, 128 * i + 128, T["wt%d" % b][:, 512 * i:512 * i + 512], *d)
-            if i == 3:
-                k["qw%d" % b] = t
-            yield 1
-
-    def side_v():
-        k["qv"] = quant("V", 0, NP, T.vt[:], *dw[L].values())
-        yield 1
-
-    def gauges():
-        for j in (1, 2):
-            gg[j] = gauge(j)
-        yield 1
-        qg[1] = quant("G1", 0, NP, T.gt1[:], gg[1])
-        yield 1
-
-    def own_list(b):
-        n = "%d" % b
-        sm, su, cc = T["sm" + n], T["su" + n], T["cc" + n]
-        k["wa"] = V(lambda q: q.tensor_scalar(T["wa" + n][:], T.ps[:, 0:NP], 0.0, None, A.is_lt), k["sc"])
-        yield 1
-        k["ct"] = V(lambda q: q.tensor_tensor_scan(cc[:], T["wa" + n][:], T["wa" + n][:], NP - 1.0, A.add, A.max), k["wa"])
-        ccs.append(k["ct"])
-        sums = [S(lambda q: q.activation(T["jk" + n][:, NP * c:NP * c + NP], cc[:], F.Sign, bias=T.pj[:, 8 + c:9 + c], scale=-1.0,
-                                         accum_out=su[:, c:c + 1]), k["ct"], kjb) for c in range(3)]
-        yield 1
-        for c in range(3):
-            t = V(lambda q: q.tensor_scalar(sm[:, c:c + 1], cc[:, NP - 1:NP], T.pj[:, 16 + c:17 + c], T.pj[:, c:c + 1], A.is_le, A.mult),
-                  k["ct"], kjc)
-        yield 1
-        t = V(lambda q: q.tensor_scalar(sm[:, 8:11], sm[:, 0:3], 64.0, None, A.add), t)
-        yield 1
-        for c in range(3):
-            z = V(lambda q: q.tensor_scalar(T["zz" + n][:, c:c + 1], su[:, c:c + 1], 0.5, sm[:, 8 + c:9 + c], A.mult, A.add), t, sums[c])
-        az.append(send(peers[b], T["lz" + n][:, 0:3], T["zz" + n][:, 0:3], "az" + n, z, quiet=(b == 1)))
-        yield 1
-        lo = k["lo"] = V(lambda q: q.tensor_scalar(T["lo" + n][:, 0:3], T["zz" + n][:, 0:3], float(NP - 1), None, A.min), z)
-        yield 1
-        k["xc"] = pick_c("X" + n, NP, WIN, "A" + n, NP, "lo" + n, 3, lo, Ac)
-        k["xs"] = pick_s("X" + n, NP, WIN, "A" + n, NP, "lo" + n, 3, lo, As)
-        yield 1
-
-    def merging_list(b):
-        n = "%d" % b
-        sm, cc = T["sm" + n], T["cc" + n]
-        k["wd"] = V(lambda q: q.tensor_tensor(T["wd" + n][:], T.ps[:, 0:NP], T.th[:], A.is_lt), k["sc"], th)
-        yield 1
-        t = V(lambda q: q.tensor_tensor(T["yd" + n][:], T["wd" + n][:], cc[:], A.mult), k["wd"], k["ct"])
-        yield 1
-        t = V(lambda q: q.tensor_tensor_scan(T["dd" + n][:], T.rm[:], T["yd" + n][:], 0.0, A.mult, A.add), t, rm)
-        yield 1
-        d8 = T["dd" + n][:, 15:128:16]
-        t = V(lambda q: q.tensor_scalar(sm[:, 16:24], d8, float(WIN - 1), None, A.is_le), t)
-        yield 1
-        t = V(lambda q: q.tensor_tensor(sm[:, 24:32], sm[:, 16:24], d8, A.mult), t)
-        yield 1
-        t = V(lambda q: q.tensor_tensor(sm[:, 32:40], sm[:, 24:32], T.pj[:, 0:8], A.max), t, kp8)
-        yield 1
-        k["ml"] = V(lambda q: q.tensor_copy(T["ml" + n][:], sm[:, 32:40]), t)
-        if b == 1:
-            t = V(lambda q: q.tensor_scalar(sm[:, 40:44], sm[:, 32:36], 256.0, None, A.mult), t)
-            yield 1
-            t = V(lambda q: q.tensor_tensor(sm[:, 44:48], sm[:, 40:44], sm[:, 36:40], A.add), t)
-            yield 1
-            t = V(lambda q: q.tensor_copy(T.mx1[:], sm[:, 44:48]), t)
-            k["aml"] = send(peers[2], T.mxl[:], T.mx1[:], "aml", t)
-        yield 1
-
-    def send_numbers():
-        base = float(NP * (rank & ~1))
-        t = V(lambda q: q.transpose(T.it[:, 0:NP], T.im1[:, 0:NP]), ids)
-        yield 1
-        t = V(lambda q: q.tensor_scalar(T.pa[:, 0:2], T.it[:, 0:64:32], 256.0, -257.0 * base, A.mult, A.add), t)
-        yield 1
-        t = V(lambda q: q.tensor_tensor(T.pa[:, 4:6], T.pa[:, 0:2], T.it[:, 64:128:32], A.add), t)
-        yield 1
-        t = V(lambda q: q.tensor_copy(T.px[:, 0:2], T.pa[:, 4:6]), t)
-        k["ai1"] = send(peers[1], T.pl[:, 0:2], T.px[:, 0:2], "ai1", t, quiet=True)
-        yield 1
-
-    def take_numbers():
-        base = float(NP * ((rank ^ 2) & ~1))
-        e = V(lambda q: q.tensor_copy(T.ui[:, 0:2], T.pl[:, 0:2]), k["ai1"])
-        yield 1
-        e1 = V(lambda q: q.tensor_scalar(T.uj[:, 0:2], T.ui[:, 0:2], 8, None, A.logical_shift_right), e)
-        e2 = V(lambda q: q.tensor_scalar(T.uj[:, 4:6], T.ui[:, 0:2], 255, None, A.bitwise_and), e)
-        yield 1
-        e1 = V(lambda q: q.tensor_scalar(T.ex[:, 0:64:32], T.uj[:, 0:2], base, None, A.add), e1, zx)
-        e2 = V(lambda q: q.tensor_scalar(T.ex[:, 64:128:32], T.uj[:, 4:6], base, None, A.add), e2)
-        yield 1
-        idp = V(lambda q: q.transpose(T.iw1[:, 0:NP], T.ex[:, 0:NP]), e1, e2)
-        idn = pick_n(T.im1[:, NP:WIN], "iw1", WIN, "lz1", 3, idp, idw, az[1])
-        k["ids"] = pick_n(T.im2[:, 0:NP], "im1", WIN, "ml1", 8, idn, ids, old)
-        yield 1
-        e = V(lambda q: q.transpose(T.it[:, NP:2 * NP], T.im2[:, 0:NP]), k["ids"])
-        yield 1
-        e = V(lambda q: q.tensor_copy(T.qx[:], T.it[:, NP:2 * NP:32]), e)
-        k["ai2"] = send(peers[2], T.ql[:], T.qx[:], "ai2", e)
-        yield 1
-
-    def take_list():
-        e = V(lambda q: q.tensor_copy(T.ui[:, 4:8], T.mxl[:]), k["aml"])
-        yield 1
-        e1 = V(lambda q: q.tensor_scalar(T.uj[:, 8:12], T.ui[:, 4:8], 8, None, A.logical_shift_right), e)
-        e2 = V(lambda q: q.tensor_scalar(T.uj[:, 12:16], T.ui[:, 4:8], 255, None, A.bitwise_and), e)
-        yield 1
-        e1 = V(lambda q: q.tensor_copy(T.pm[:, 0:4], T.uj[:, 8:12]), e1)
-        k["pm"] = V(lambda q: q.tensor_copy(T.pm[:, 4:8], T.uj[:, 12:16]), e2)
-        yield 1
-
-    def new_columns(b):
-        n = "%d" % b
-        h = T["ht" + n]
-        Pd = (P,)
-        if b == 2:
-            Pd = (pick_c("P2", 0, NP, "R", WIN, "pm", 8, k["pm"], ar0, ar1), pick_s("P2", 0, NP, "R", WIN, "pm", 8, k["pm"], ar0, ar1))
-        mm = [E(lambda q: q.matmul_mx(T.pe[:, 512 * i:512 * i + NP], T["cW" + n][:, 128 * i:128 * i + 128], T["sW" + n][:, 128 * i:128 * i + 128],
-                                      T["cP" + n][:, 0:NP], T["sP" + n][:, 0:NP], True, True), k["qw" + n], casts[i], *Pd) for i in range(4)]
-        for i in range(3):
-            casts[i] = S(lambda q: q.activation(h[:, i:512:4], T.pe[:, 512 * i:512 * i + NP], F.Copy, scale=0.0625), mm[i])
-        yield 1
-        casts[3] = V(lambda q: q.tensor_scalar(h[:, 3:512:4], T.pe[:, 1536:1536 + NP], 0.0625, None, A.mult), mm[3])
-        yield 1
-        k["qn"] = quant("X" + n, 0, NP, h[:], *casts)
-        yield 1
-
-    for b in range(L):
-        n = "%d" % b
-        if b == 1:
-            ids = pick_n(T.im1[:, 0:NP], "im0", WIN, "ml0", 8, idn, ids, k["ml"])
-        k["sc"] = E(lambda q: q.matmul_mx(T.ps[:, 0:NP], T["cG" + n][:, 0:NP], T["sG" + n][:, 0:NP], T["cA" + n][:, 0:NP],
-                                          T["sA" + n][:, 0:NP], True, True), qg[b], Ac, As, k["wa"], k["wd"])
-        old = k["ml"]
-        if b == 0:
-            turns(ORDER[0], o=own_list(0), m=merging_list(0), g=gauges(), e=expert(0), n=new_columns(0))
-            point("p0", P)
-            qg[2] = quant("G2", 0, NP, T.gt2[:], gg[2])
-        if b == 1:
-            turns(ORDER[1], e=expert(1), o=own_list(1), s=send_numbers(), m=merging_list(1), n=new_columns(1), v=side_v())
-            last = expert(2)
-            next(last)
-        if b == 2:
-            turns(ORDER[2], e=last, t=take_numbers(), o=own_list(2), l=take_list(), n=new_columns(2), m=merging_list(2))
-            ids, ai2 = k["ids"], k["ai2"]
-        idw = pick_n(T["iw" + n][:, NP:WIN], "im" + n, NP, "lo" + n, 3, k["lo"], ids)
-        if b == 0:
-            idn = pick_n(T.im0[:, NP:WIN], "iw0", WIN, "lz0", 3, idp, idw, az[0])
-        if b == 2:
-            for j in range(L):
-                count(j)
-        nc = pick_c("M" + n, NP, WIN, "X" + n, WIN, "lz" + n, 3, k["qn"], k["xc"], az[b])
-        ns = pick_s("M" + n, NP, WIN, "X" + n, WIN, "lz" + n, 3, k["qn"], k["xs"], az[b])
-        if b == 1:
-            send_codes(peers[2], "R", "M1", NP, WIN, "ar1", nc)
-            ar1 = send_scales(peers[2], "R", "M1", NP, WIN, "ar1", ns)
-        o = "%d" % (b + 1)
-        Ac = pick_c("A" + o, 0, NP, "M" + n, WIN, "ml" + n, 8, nc, k["ml"], Mc)
-        As = pick_s("A" + o, 0, NP, "M" + n, WIN, "ml" + n, 8, ns, k["ml"], Ms)
-        if b == 0:
-            send_codes(peers[1], "P1", "A1", 0, NP, "ap1", Ac)
-            P = send_scales(peers[1], "P1", "A1", 0, NP, "ap1", As)
-        if b < 2:
-            sent = issued()
-            load("y", "dm" + n, T["cM" + o][:, 0:NP].bitcast(dt.uint8), T["cA" + o][:, 0:NP].bitcast(dt.uint8), Ac, sent)
-            Mc = Ms = load("y", "dm" + n, T["sM" + o][:, 0:NP], T["sA" + o][:, 0:NP], As)
-        if b == 0:
-            send_codes(peers[2], "R", "A1", 0, NP, "ar0", Ac)
-            ar0 = send_scales(peers[2], "R", "A1", 0, NP, "ar0", As)
-
-    ym = E(lambda q: q.matmul_mx(T.py[:, 0:NP], T.cV[:, 0:NP], T.sV[:, 0:NP], T.cA3[:, 0:NP], T.sA3[:, 0:NP], True, True), k["qv"], Ac, As)
-    load("y", "out", T.oc[:, 0:4 * NP], T.cA3[:, 0:NP].bitcast(dt.uint8), Ac)
-    for j in range(4):
-        load("y", "out", T.osc[4 * j:4 * j + 4, 0:NP], T.sA3[32 * j:32 * j + 4, 0:NP], As)
-    kk = [V(lambda q: q.tensor_scalar(T.kk[:, 4 + b:5 + b], T.kk[:, b:b + 1], NP - 1.0, T["cc%d" % b][:, NP - 1:NP], A.add, A.min), kp[b], ccs[b])
-          for b in range(L)][-1]
-    e = V(lambda q: q.tensor_copy(T.ex[:, NP:2 * NP:32], T.ql[:]), ai2, zx)
-    kk = V(lambda q: q.tensor_scalar(T.kk[:, 8:8 + L], T.kk[:, 4:4 + L], 1.0 - NP, None, A.add), kk)
-    idp = V(lambda q: q.transpose(T.iw2[:, 0:NP], T.ex[:, NP:2 * NP]), e)
-    yt = V(lambda q: q.tensor_copy(T.yt[:], T.py[:, 0:NP]), ym)
-    load("y", "out", T.y[:], T.yt[:], yt)
-    load("y", "out", T.ks[:], T.kk[0:1, 8:8 + L], kk)
-    idn = pick_n(T.im2[:, NP:WIN], "iw2", WIN, "lz2", 3, idp, idw, az[2])
-    idf = pick_n(T.idf[:], "im2", WIN, "ml2", 8, idn, ids, k["ml"])
-    load("y", "out", T.ids[:], T.idf[0:1, :], idf)
-
+    for i in ORDER or range(len(ops)):
+        o = ops[i]
+        marks = {}
+        for j in o["need"]:
+            for s, n in done[j]:
+                marks[s] = max(marks.get(s, 0), n)
+        for s in sorted(marks):
+            wait(o["q"], s, marks[s])
+        call = o["call"](queue[o["q"]])
+        if o["more"] is None:
+            call.then_inc(T.sem[o["sem"]], o["n"])
+        adds = {o["sem"]: o["n"], **(o["more"] or {})}
+        for s in adds:
+            total[s] = total.get(s, 0) + adds[s]
+        done[i] = [(s, total[s]) for s in adds if s != "sent"]
     for s in sorted(total):
-        need("g", [(s, total[s])])
+        wait("g", s, total[s])

from concourse.mybir import dt, AluOpType, ActivationFunctionType

L, CAPP, NP = 3, 48, 128
WIN = NP + CAPP
SEG = NP + 1
CUT = 88
LOW = 2048.0
A = AluOpType
F = ActivationFunctionType
LOADS = [(0, 0, 2, None), (0, 2, 2, None), (1, 0, 4, None), (3, 0, 1, None), (2, 0, 4, "ap0s")]
CASTS = "svsvsvsvsvsvv"
OUTS = "yyyyssyy"
AGAIN = ("nw0", "nw1", "nw2")
ORDER = [10, 1, 6, 0, 9, 7, 2, 3, 15, 4, 8, 16, 29, 13, 11, 18, 17, 27, 35, 12, 20, 19, 36, 14, 38, 37, 32, 39, 31, 48, 43, 49, 40, 23, 53, 22, 41, 55, 72, 21, 25, 34, 52, 56, 30, 24, 42, 74, 28, 44, 59, 57, 47, 58, 26, 46, 63, 33, 60, 45, 71, 73, 61, 64, 125, 50, 62, 67, 68, 66, 65, 77, 54, 76, 5, 75, 78, 81, 80, 79, 82, 88, 69, 90, 83, 70, 84, 85, 51, 86, 87, 126, 89, 127, 91, 98, 124, 99, 92, 96, 102, 112, 101, 93, 100, 111, 97, 170, 103, 94, 167, 104, 171, 117, 129, 105, 128, 130, 131, 133, 132, 121, 95, 134, 120, 135, 113, 119, 118, 122, 136, 169, 123, 137, 138, 106, 141, 139, 142, 107, 145, 110, 109, 140, 108, 168, 148, 143, 149, 144, 159, 114, 158, 150, 152, 151, 115, 146, 153, 116, 147, 154, 155, 172, 160, 164, 173, 192, 163, 161, 162, 165, 174, 175, 176, 177, 178, 179, 180, 181, 166, 189, 182, 156, 183, 184, 193, 157, 185, 186, 194, 187, 195, 198, 190, 196, 199, 197, 191, 188, 200, 201]

SCRATCH = {}


def _mx(name, n):
    SCRATCH["c" + name] = ("sbuf", [128, n], "float8_e4m3fn_x4")
    SCRATCH["s" + name] = ("sbuf", [128, n], "uint8")


def _sb(name, n, dtype="float32"):
    SCRATCH[name] = ("sbuf", [128, n], dtype)


for _b in range(L):
    _mx("A%d" % _b, NP)
    _mx("M%d" % _b, WIN)
    _mx("X%d" % _b, WIN)
    _mx("G%d" % _b, NP)
    _mx("W%d" % _b, 512)
    _mx("P%d" % _b, NP)
    _sb("wt%d" % _b, 2048, "bfloat16")
    _sb("gt%d" % _b, 512, "bfloat16")
    _sb("ht%d" % _b, 512, "bfloat16")
    _sb("nw%d" % _b, NP, "bfloat16")
    _sb("co%d" % _b, 3 * SEG, "bfloat16")
    _sb("zz%d" % _b, 8, "uint16")
    _sb("lo%d" % _b, 4, "uint16")
    _sb("lz%d" % _b, 8, "uint16")
    _sb("im%d" % _b, WIN)
    _sb("iw%d" % _b, WIN)
for _b in range(L + 1):
    _sb("mr%d" % _b, WIN, "bfloat16")
    _sb("me%d" % _b, NP, "bfloat16")
    _sb("ml%d" % _b, 8, "uint16")
_mx("A3", NP)
_mx("R", WIN)
_mx("H", NP)
_mx("V", NP)
_sb("xt", 512, "bfloat16")
_sb("ut", 4 * L, "bfloat16")
_sb("vt", 512, "bfloat16")
_sb("zb", SEG, "bfloat16")
_sb("tc", WIN, "bfloat16")
_sb("ct", 3 * SEG, "bfloat16")
_sb("dd", 3 * L * SEG, "bfloat16")
_sb("ia", NP, "int32")
_sb("ib", NP, "int32")
_sb("iq", 4, "int32")
_sb("cs", 8)
_sb("k16", 3 * NP, "bfloat16")
_sb("k128", 2 * SEG, "bfloat16")
_sb("cw", WIN, "bfloat16")
_sb("kj", CAPP * L, "bfloat16")
_sb("ie", SEG)
_sb("it", NP)
_sb("ex", NP)
_sb("lp", 4, "uint16")
_sb("e1", 32)
_sb("idf", NP)
_sb("kk", 12)
_sb("yt", NP)
SCRATCH["pe"] = ("psum", [128, 2048], "float32")
SCRATCH["ps"] = ("psum", [128, 512], "float32")
SCRATCH["py"] = ("psum", [128, 512], "float32")

SEMAPHORES = (["v", "s", "t", "g", "sent", "out", "dx", "du"] + ["dw%d" % i for i in range(len(LOADS))]
              + ["dm%d%s" % (b, c) for b in range(1, L) for c in "cs"] + ["ap%d%s" % (b, c) for b in range(L - 1) for c in "cs"]
              + ["ahc", "ahs", "hrc", "hrs", "arc", "anc", "ans", "az0", "az1", "az2", "alp"])


def helper(c, T, topo):
    mine = [e for e in T.cores if topo.chip(e) == topo.chip(c)]
    free = [e for e in topo.cores_of(c) if topo.die(e) != topo.die(c) and e not in T.cores]
    return free[mine.index(c)]


def engines(src, dst, far, quiet, topo):
    return [e for e in topo.engines(src, dst) if not quiet or e not in topo.engines(src, far)]


def bits(es):
    return sum(1 << e for e in es)


def build(core, T, topo):
    rank = T.rank_of(core)
    peers = [T.cores[rank ^ (1 << b)] for b in range(L)]
    ops, seen, named = [], {}, {}

    def p(name, a=0, b=None, step=1, off=None):
        return (name, a, T[name].shape[1] if b is None else b, step, off)

    def by(name, n, off, k):
        return p(name, 0, n, 1, p(off, 0, k))

    def view(x, word=None):
        if not isinstance(x, tuple):
            return x
        v = T[x[0]][:, x[1]:x[2]:x[3]] if x[3] > 1 else T[x[0]][:, x[1]:x[2]]
        if word is not None and SCRATCH[x[0]][2] == "float8_e4m3fn_x4":
            v = v.bitcast(word)
        return v if x[4] is None else v.indirect(view(x[4]))

    def op(q, call, outs, ins, sem=None, n=1, name=None, after=(), more=None):
        me, need = len(ops), set(named[a] for a in after if a is not None)
        ins = [x for x in ins if isinstance(x, tuple)]
        ins += [x[4] for x in outs + ins if x[4] is not None]
        for xs, w in ((ins, False), (outs, True)):
            for x in xs:
                bank = SCRATCH[x[0]][0] == "psum"
                cols = set(range(x[1] // 512 * 512, x[1] // 512 * 512 + 512) if bank else range(x[1], x[2], x[3]))
                for j, c2, w2 in seen.setdefault(x[0], []):
                    if j != me and (w or w2 or (bank and ops[j]["q"] != q)) and cols & c2:
                        need.add(j)
                seen[x[0]].append((me, cols, w))
        ops.append({"q": q, "call": call, "need": need, "sem": sem or q, "n": n, "name": name, "more": more})
        name = name or outs[0][0]
        if name not in named:
            named[name] = me
            loads(name)

    def ts(out, in0, s1, s2, *alu):
        op("v", lambda e: e.tensor_scalar(view(out), view(in0), view(s1), view(s2), *alu), [out], [in0, s1, s2])

    def tt(out, in0, in1, alu):
        op("v", lambda e: e.tensor_tensor(view(out), view(in0), view(in1), alu), [out], [in0, in1])

    def scan(out, d0, d1, init, op0, op1):
        op("v", lambda e: e.tensor_tensor_scan(view(out), view(d0), view(d1), view(init), op0, op1), [out], [d0, d1, init])

    def copy(out, in_):
        op("v", lambda e: e.tensor_copy(view(out, dt.uint32), view(in_, dt.uint32)), [out], [in_])

    def fill(out, c):
        op("v", lambda e: e.memset(view(out), c), [out], [])

    def turn(out, in_):
        op("v", lambda e: e.transpose(view(out), view(in_)), [out], [in_])

    def quant(to, a, b, in_):
        c, s = p("c" + to, a, b), p("s" + to, a, b)
        op("v", lambda e: e.quantize_mx(view(c), view(s), view(in_)), [c, s], [in_])

    def act(out, in_, func=F.Copy, **kw):
        op("s", lambda e: e.activation(view(out), view(in_), func, **{a: view(x) for a, x in kw.items()}),
           [out] + [x for a, x in kw.items() if a == "accum_out"], [in_] + [x for a, x in kw.items() if a != "accum_out"])

    def iota(out, pattern, base, mult, **kw):
        op("g", lambda e: e.iota(view(out), pattern, base, mult, **kw), [out], [])

    def choose(out, in_, value, base):
        op("g", lambda e: e.affine_select(view(out), view(in_), [[1, SEG]], A.not_equal, value, base, -1), [out], [in_])

    def product(out, w, a, x):
        ins = [p("c" + w, a, a + NP), p("s" + w, a, a + NP), p("c" + x, 0, NP), p("s" + x, 0, NP)]
        op("t", lambda e: e.matmul_mx(view(out), *[view(i) for i in ins], True, True), [out], ins)

    def dma(q, sem, out, in_, outs, ins, after=()):
        op(q, lambda e: e.dma_start(out, in_), outs, ins, sem=sem, n=16, name=sem, after=after)

    def send(dst, out, in_, sem, quiet=False):
        es = engines(core, dst, peers[2], quiet, topo)
        rid, pid, _ = topo.addr(dst)
        op("g", lambda e: e.remote_dma(view(out, dt.uint8), view(in_, dt.uint8), T.sem[sem], T.sem["sent"], pid, rid, bits(es)),
           [out], [in_], sem=sem, n=len(es), name=sem, more={"sent": len(es)})

    def send_by_helper(k, a):
        hc = helper(core, T, topo)
        es = engines(core, hc, peers[2], k == "s", topo)
        rid, pid, _ = topo.addr(hc)
        op("g", lambda e: e.remote_dma(view(p(k + "H", a, NP), dt.uint8), view(p(k + "A1", a, NP), dt.uint8), T.sem["ah" + k], T.sem["sent"], pid, rid, bits(es)),
           [p(k + "R", a, NP)], [p(k + "A1", a, NP)], sem="hr" + k, n=len(topo.engines(hc, peers[2])), name="hr" + k, more={"sent": len(es)})

    def pick(to, a, b, frm, n, off):
        copy(p("c" + to, a, b), by("c" + frm, n, off, (b - a) // 16))
        act(p("s" + to, a, b), by("s" + frm, n, off, (b - a) // 16))

    def again(b):
        for c in "cs":
            o, i = p(c + "M%d" % b, 0, NP), p(c + "A%d" % b)
            dma("y", "dm%d%s" % (b, c), view(o, dt.uint8), view(i, dt.uint8), [o], [i], [AGAIN[b]])

    def merging(b, off):
        n = "%d" % b
        copy(by("mr" + n, WIN, off, 3), p("tc", NP, WIN))
        scan(p("me" + n), p("k16", 0, NP), p("mr" + n, 0, NP), 0.0, A.add, A.min)
        ts(p("ml" + n), p("me" + n, 15, NP, 16), p("cs", 1, 2), None, A.add)

    def loads(name):
        for i, (b, j, w, after) in enumerate(LOADS):
            if after != name:
                continue
            if b == L:
                dma("y", "dw%d" % i, T.vt[:], T.v[:], [p("vt")], [], [after])
            else:
                o = p("wt%d" % b, 512 * j, 512 * (j + w))
                dma("y", "dw%d" % i, view(o), T.w[:, 2048 * b + 512 * j:2048 * b + 512 * (j + w)], [o], [], [after])

    dma("y", "dx", T.xt[:], T.x[:], [p("xt")], [])
    dma("s", "du", T.ut[:], T.u[:, 0:4 * L], [p("ut")], [])
    loads(None)
    flag = {"allow_small_or_imprecise_dtypes": True}
    iota(p("iq", 0, 2), [[0, 2]], 0, 1)
    iota(p("tc"), [[1, WIN]], 0, 0, **flag)
    iota(p("ia"), [[1, NP]], NP, -1)
    fill(p("zb"), 0.0)
    fill(p("dd", NP, None, SEG), -1.0)
    act(p("ex"), p("tc", 0, NP), scale=0.0)
    act(p("iw1", 0, NP), p("tc", 0, NP), scale=0.0)
    act(p("e1"), p("tc", 0, 32), scale=0.0)
    act(p("im1", NP, WIN), p("tc", 0, CAPP), scale=0.0)
    ts(p("iq", 2, 3), p("iq", 0, 1), 15, None, A.bitwise_and)
    ts(p("cs", 0, 1), p("iq", 2, 3), 1.0, None, A.add)
    ts(p("cs", 1, 2), p("cs", 0, 1), 16.0, 256.0, A.is_lt, A.mult)
    ts(p("cs", 4, 7), p("tc", 0, CAPP, 16), p("cs", 0, 1), None, A.add)
    for c in range(3):
        act(p("ct", SEG * c, SEG * c + NP), p("tc", 0, NP), scale=1.0 / 256)
    ts(p("ct", NP, None, SEG), p("cs", 4, 7), NP - 1.0, 1.0 / 256, A.add, A.mult)
    ts(p("ib"), p("ia", 0, NP), 15, None, A.bitwise_and)
    ts(p("k16", NP, 2 * NP), p("ib"), 0.0, 1024.0, A.is_equal, A.mult)
    ts(p("k16", 2 * NP, 3 * NP), p("ib"), 1.0, -256.0, A.is_equal, A.mult)
    tt(p("k16", 0, NP), p("k16", NP, 2 * NP), p("k16", 2 * NP, 3 * NP), A.add)
    choose(p("k128", SEG, 2 * SEG), p("zb", 0, SEG), 4 * LOW, 0)
    choose(p("k128", 0, SEG), p("k128", SEG, 2 * SEG), -LOW, -1)
    ts(p("cw"), p("tc"), float(NP), None, A.is_lt)
    for b in range(L + 1):
        act(p("mr%d" % b), p("tc"))
    act(p("im0", 0, NP), p("tc", 0, NP), F.Identity, bias=float(rank * NP))
    act(p("iw0", 0, NP), p("tc", 0, NP), F.Identity, bias=float((rank ^ 1) * NP))
    for t in range(4):
        ts(p("gt0", t, 512, 4), p("zb", 0, NP), p("ut", t, t + 1), None, A.add)
    for b in (1, 2):
        for t in range(4):
            act(p("gt%d" % b, t, 512, 4), p("zb", 0, NP), F.Identity, bias=p("ut", 4 * b + t, 4 * b + t + 1))
    quant("A0", 0, NP, p("xt"))
    for b in range(L):
        quant("G%d" % b, 0, NP, p("gt%d" % b))

    for b in range(L):
        n, o = "%d" % b, "%d" % (b + 1)
        if b < 2:
            for c in "cs":
                send(peers[b], p(c + "P" + n), p(c + "A" + n), "ap" + n + c)
        if b == 1:
            send_by_helper("c", CUT)
            send(peers[2], p("cR", 0, CUT), p("cA1", 0, CUT), "arc")
            send_by_helper("s", 0)
            scan(p("ie"), p("k128", 0, SEG), p("im1", 0, SEG), 0.0, A.add, A.min)
            ts(p("zz1", 3, 4), p("ie", NP, SEG), LOW, None, A.add)
        if b == 2:
            turn(p("it"), p("im2", 0, NP))
            copy(p("zz2", 3, 7), p("it", 0, NP, 32))
        product(p("ps", 0, NP), "G" + n, 0, "A" + n)
        ts(p("nw" + n), p("ps", 0, NP), 0.0, -1.0, A.is_lt, A.mult)
        d = 3 * SEG * b
        for c in range(3):
            scan(p("dd", d + SEG * c, d + SEG * c + NP), p("nw" + n), p("zb", 0, NP), p("cs", 4 + c, 5 + c), A.add, A.add)
        scan(p("co" + n), p("ct"), p("dd", d, d + 3 * SEG), 1.0, A.min, A.max)
        ts(p("zz" + n, 0, 3), p("co" + n, NP, None, SEG), 256.0, None, A.mult)
        send(peers[b], p("lz" + n, 0, (3, 4, 7)[b]), p("zz" + n, 0, (3, 4, 7)[b]), "az" + n, b == 1)
        if b == 1:
            copy(p("e1", 0, 1), p("lz1", 3, 4))
            for a in range(0, NP, 32):
                op("v", lambda e, a=a: e.transpose(T.iw1[0:32, a:a + 32], T.e1[a:a + 32, 0:32]), [p("iw1", a, a + 32)], [p("e1")])
        if b == 2:
            copy(p("ex", 0, NP, 32), p("lz2", 3, 7))
            turn(p("iw2", 0, NP), p("ex"))
        if b:
            again(b)
        else:
            quant("M0", 0, NP, p("xt"))
        if b == 1:
            send(peers[2], p("lp", 0, 3), p("zz1", 0, 3), "alp")
            merging(L, "lp")
        ts(p("lo" + n, 0, 3), p("co" + n, NP, None, SEG), 256.0, NP - 1.0, A.mult, A.min)
        pick("X" + n, NP, WIN, "A" + n, NP, "lo" + n)
        act(p("iw" + n, NP, WIN), by("im" + n, NP, "lo" + n, 3))
        merging(b, "zz" + n)
        for i in range(4):
            quant("W" + n, NP * i, NP * i + NP, p("wt" + n, 512 * i, 512 * i + 512))
        if b == 2:
            quant("V", 0, NP, p("vt"))
            pick("P2", 0, NP, "R", WIN, "ml3")
        for i in range(4):
            product(p("pe", 512 * i, 512 * i + NP), "W" + n, NP * i, "P" + n)
        for i in range(4):
            h, r = p("ht" + n, i, 512, 4), p("pe", 512 * i, 512 * i + NP)
            if CASTS[4 * b + i] == "v":
                ts(h, r, 0.0625, None, A.mult)
            else:
                act(h, r, scale=0.0625)
        quant("X" + n, 0, NP, p("ht" + n))
        pick("M" + n, NP, WIN, "X" + n, WIN, "lz" + n)
        if b == 1:
            for c in "cs":
                send(peers[2], p(c + "R", NP, WIN), p(c + "M1", NP, WIN), "an" + c)
        pick("A" + o, 0, NP, "M" + n, WIN, "ml" + n)
        act(p("im" + n, NP, WIN), by("iw" + n, WIN, "lz" + n, 3))
        act(p("im" + o, 0, NP) if b < 2 else p("idf"), by("im" + n, WIN, "ml" + n, 8))
        act(p("kj", CAPP * b, CAPP * b + CAPP), by("cw", WIN, "lz" + n, 3), accum_out=p("kk", b, b + 1))

    product(p("py", 0, NP), "V", 0, "A3")
    (copy if CASTS[4 * L] == "v" else act)(p("yt"), p("py", 0, NP))
    ts(p("kk", 4, 4 + L), p("dd", NP - 1, None, 3 * SEG), -1.0, 1.0, A.mult, A.add)
    tt(p("kk", 8, 8 + L), p("kk", 4, 4 + L), p("kk", 0, L), A.min)
    dma(OUTS[0], "out", T.ks[:], T.kk[0:1, 8:8 + L], [], [p("kk", 8, 8 + L)])
    dma(OUTS[1], "out", T.oc[:, 0:4 * NP], view(p("cA3"), dt.uint8), [], [p("cA3")])
    for j in range(4):
        dma(OUTS[2 + j], "out", T.osc[4 * j:4 * j + 4, 0:NP], T.sA3[32 * j:32 * j + 4, 0:NP], [], [p("sA3")])
    dma(OUTS[6], "out", T.y[:], T.yt[:], [], [p("yt")])
    dma(OUTS[7], "out", T.ids[:], T.idf[0:1, :], [], [p("idf")])
    return ops


def rank_program(g, core, T, topo):
    if T.rank_of(core) is None:
        for r, c in enumerate(T.cores):
            if helper(c, T, topo) == core:
                dst = T.cores[r ^ (1 << (L - 1))]
                rid, pid, _ = topo.addr(dst)
                off = topo.engines(core, dst)
                g.wait_ge(T.sem["ahc"], len(engines(c, core, dst, False, topo)))
                g.remote_dma(T.cR[:, CUT:NP].bitcast(dt.uint8), T.cH[:, CUT:NP].bitcast(dt.uint8), T.sem["hrc"], T.sem["sent"], pid, rid, bits(off))
                g.wait_ge(T.sem["ahs"], len(engines(c, core, dst, True, topo)))
                g.remote_dma(T.sR[:, 0:NP], T.sH[:, 0:NP], T.sem["hrs"], T.sem["sent"], pid, rid, bits(off))
                g.wait_ge(T.sem["sent"], 2 * len(off))
        return
    ops = build(core, T, topo)
    queue = {"v": g.vector, "s": g.scalar, "t": g.tensor, "g": g, "y": g.sync}
    total, known, done = {}, {q: {} for q in queue}, {}

    def wait(q, s, n):
        if known[q].get(s, 0) < n:
            queue[q].wait_ge(T.sem[s], n)
            known[q][s] = n

    for i in ORDER or range(len(ops)):
        o = ops[i]
        marks = {}
        for j in o["need"]:
            for s, n in done[j]:
                marks[s] = max(marks.get(s, 0), n)
        for s in sorted(marks):
            wait(o["q"], s, marks[s])
        call = o["call"](queue[o["q"]])
        if o["more"] is None:
            call.then_inc(T.sem[o["sem"]], o["n"])
        adds = {o["sem"]: o["n"], **(o["more"] or {})}
        for s in adds:
            total[s] = total.get(s, 0) + adds[s]
        done[i] = [(s, total[s]) for s in adds if s != "sent"]
    for s in sorted(total):
        wait("g", s, total[s])
